import numpy as np
import ml_dtypes


def mxq(x, axis, fmt="e4m3"):
    dtype, down = {"e4m3": (ml_dtypes.float8_e4m3fn, 7), "e5m2": (ml_dtypes.float8_e5m2, 14)}[fmt]
    v = np.moveaxis(np.asarray(x, np.float32).astype(ml_dtypes.bfloat16).astype(np.float64), axis, -1)
    blocks = v.reshape(v.shape[:-1] + (-1, 32))
    amax = np.abs(blocks).max(-1, keepdims=True)
    byte = np.maximum(np.where(amax > 0, np.frexp(amax)[1] - 1 + 127, 0) - down, 1)
    scale = np.exp2(byte - 127.0)
    codes = (blocks / scale).astype(np.float32).astype(dtype).astype(np.float64)
    return np.moveaxis((codes * scale).reshape(v.shape), -1, axis)


WIDE = False


def mx_kscale(k):
    if not WIDE:
        return np.ones(k)
    levels = np.array([10, -10, 5, -5, 0])
    if k % 512:
        return np.exp2(np.random.permutation(np.resize(levels, k // 32))).repeat(32)
    a = np.empty((k // 512, 16))
    for p in range(k // 512):
        a[p, :8] = np.random.permutation(np.resize(levels, 8))
        for g in range(8):
            far = levels[np.abs(levels - a[p, g]) >= 10]
            a[p, g + 8] = far[np.random.randint(len(far))]
    return np.exp2(a.ravel()).repeat(32)


def f64(x):
    return np.asarray(x).astype(np.float64)


def striped(idx):
    return np.tile(idx.reshape(-1, 16).T, (8, 1)).astype(np.uint16)


def unstriped(offs):
    return offs[:16].T.reshape(-1).astype(np.int64)


E2M1 = np.array([0.0, 0.5, 1.0, 1.5, 2.0, 3.0, 4.0, 6.0, -0.0, -0.5, -1.0, -1.5, -2.0, -3.0, -4.0, -6.0])


def pack_weight(w, fmt):
    k, n = w.shape
    w = f64(np.asarray(w, np.float32).astype(ml_dtypes.bfloat16)).reshape(k // 32, 32, n)
    amax = np.abs(w).max(1)
    if fmt == "e4m3":
        byte = np.frexp(amax)[1] - 1 + 127 - 7
    else:
        mant, ex = np.frexp(amax / 6.0)
        byte = np.where(mant > 0.5, ex, ex - 1) + 127
    byte = np.clip(np.where(amax > 0, byte, 1), 1, 254)
    scaled = (w * np.exp2(127.0 - byte)[:, None, :]).reshape(k, n).astype(np.float32)
    by_word = np.ascontiguousarray(scaled.reshape(k // 512, 128, 4, n).transpose(0, 1, 3, 2))
    if fmt == "e4m3":
        words = by_word.astype(ml_dtypes.float8_e4m3fn).view(np.uint8)
    else:
        c = by_word.astype(ml_dtypes.float4_e2m1fn).view(np.uint8) & 0xF
        words = (c[..., 0::2] | (c[..., 1::2] << 4)).reshape(k // 512, 128, 2 * n)
    return np.ascontiguousarray(words), np.ascontiguousarray(byte.astype(np.uint8).reshape(k // 512, 16, n))


def unpack_weight(words, scales, fmt):
    g, _, n = scales.shape
    words = np.ascontiguousarray(words).reshape(g, 128, n, -1)
    if fmt == "e4m3":
        vals = words.view(ml_dtypes.float8_e4m3fn).astype(np.float64)
    else:
        nib = np.empty((g, 128, n, 4), np.uint8)
        nib[..., 0::2] = words & 0xF
        nib[..., 1::2] = words >> 4
        vals = E2M1[nib]
    vals = vals * np.repeat(np.exp2(scales.astype(np.float64) - 127.0), 8, axis=1)[..., None]
    return vals.transpose(0, 1, 3, 2).reshape(g * 512, n)


def silu(v):
    return v / (1.0 + np.exp(-np.maximum(v, -700.0)))


K, T, E, C, N = 2048, 1280, 8, 256, 128
R = 2


def by_expert(wq, xq):
    return np.concatenate([wq[e].T @ xq[:, e * C:(e + 1) * C] for e in range(E)], axis=1)


def setup_inputs():
    n = np.random.standard_normal
    s = mx_kscale(K)[:, None]
    slot_token = np.concatenate([r * (T // R) + np.random.permutation(T // R)[:C // R] for e in range(E) for r in range(R)])
    w = [pack_weight(m, "e2m1") for m in n((E, K, N)) / np.sqrt(K) / s[None]]
    return {
        "xT": (n((K, T)) * s).astype(np.float32),
        "w_words": np.stack([m[0] for m in w]),
        "w_scales": np.stack([m[1] for m in w]),
        "b": (0.3 * n((N, E))).astype(np.float32),
        "offs": striped(slot_token),
    }


def reference(xT, w_words, w_scales, b, offs):
    idx = unstriped(offs)
    w = np.stack([unpack_weight(w_words[e], w_scales[e], "e2m1") for e in range(E)])
    xq = mxq(f64(xT)[:, idx], 0, "e4m3")
    y = by_expert(w, xq)
    y = silu(y + np.repeat(f64(b), C, axis=1))
    return y.reshape(N, E, R, C // R).transpose(0, 2, 1, 3).reshape(N, E * C)

@@ -1,0 +1,138 @@
+from contextlib import ExitStack
+
+import concourse.mybir as mybir
+
+K, T, E, C, N, R = 2048, 1280, 8, 256, 128, 2
+S = E * C
+FLOPS = 2 * K * N * S
+
+F32 = mybir.dt.float32
+BF16 = mybir.dt.bfloat16
+I32 = mybir.dt.int32
+U32 = mybir.dt.uint32
+U16 = mybir.dt.uint16
+U8 = mybir.dt.uint8
+FP8X4 = mybir.dt.float8_e4m3fn_x4
+FP4X4 = mybir.dt.float4_e2m1fn_x4
+ACT = mybir.ActivationFunctionType
+
+P = 128
+PACK = 4
+K_PASS = P * PACK
+PASSES = K // K_PASS
+UNIT = 256
+UNITS = T // UNIT
+U = C // R
+SHIFT_ROWS = 112
+
+
+def tile_moe_eps_lin_silu_kernel(tc, xT, w_words, w_scales, b, offs, out):
+    nc = tc.nc
+    with ExitStack() as ctx:
+        keep = ctx.enter_context(tc.tile_pool(name="keep", bufs=1))
+        psum = ctx.enter_context(tc.psum_pool(name="psum", bufs=1))
+
+        offsets = keep.tile([P, S // 16], U16, name="offsets")
+        bias = keep.tile([P, E], F32, name="bias")
+        raw = [[keep.tile([P, PACK, UNIT], F32, name="raw%d_%d" % (a, u)) for u in range(UNITS)] for a in range(PASSES)]
+        grouped = [keep.tile([P, T, PACK], BF16, name="grouped%d" % a, align_bytes=64) for a in range(PASSES)]
+        codes = [keep.tile([P, T], U32, name="codes%d" % a, align_bytes=64) for a in range(PASSES)]
+        scales = keep.tile([P, T], U8, name="scales", align_bytes=64)
+        slot_codes = [keep.tile([P, S], U32, name="slot_codes%d" % a, align_bytes=64) for a in range(PASSES)]
+        slot_scales = keep.tile([P, S], U8, name="slot_scales", align_bytes=64)
+        moved_scales = keep.tile([P, PASSES - 1, S], U8, name="moved_scales", align_bytes=64)
+        w_codes = keep.tile([P, E * PASSES, 2 * N], U8, name="w_codes", align_bytes=64)
+        w_planes = keep.tile([P, E * PASSES, N], U8, name="w_planes", align_bytes=64)
+        result = keep.tile([P, R, E * U], F32, name="result")
+        warm_in = keep.tile([P, 1], F32, name="warm_in")
+        warm_out = keep.tile([P, 1], F32, name="warm_out")
+        acc = [psum.tile([P, R, U], F32, name="acc%d" % e) for e in range(E)]
+
+        nc.vector.memset(warm_in[:], 0.0)
+        nc.scalar.activation(out=warm_out[:], in_=warm_in[:], func=ACT.Silu)
+        nc.vector.memset(scales[:].bitcast(I32), 0)
+        nc.vector.memset(w_planes[:].bitcast(I32), 0)
+        nc.vector.memset(moved_scales[:].bitcast(I32), 0)
+
+        for a in range(PASSES):
+            rows = xT[a * K_PASS:(a + 1) * K_PASS, :].rearrange("(p j) t -> p j t", j=PACK)
+            for u in range(UNITS):
+                nc.sync.dma_start(out=raw[a][u][:], in_=rows[:, :, u * UNIT:(u + 1) * UNIT])
+            if a == 0:
+                nc.sync.dma_start(offsets[:], offs)
+                nc.sync.dma_start(out=bias[:], in_=b)
+        scale_rows = w_scales.rearrange("e a q n -> q (e a) n").bitcast(I32)
+        for quad in range(4):
+            nc.sync.dma_start(out=w_planes[32 * quad:32 * quad + 4].bitcast(I32), in_=scale_rows[4 * quad:4 * quad + 4])
+        word_rows = w_words.rearrange("e a p c -> p (e a) c").bitcast(I32)
+        for pair in range(E // 2):
+            mats = slice(2 * pair * PASSES, 2 * (pair + 1) * PASSES)
+            nc.sync.dma_start(out=w_codes[:, mats, :].bitcast(I32), in_=word_rows[:, mats, :])
+
+        def cast(a, u, lo, hi, on_vector):
+            dst = grouped[a][:, u * UNIT + lo:u * UNIT + hi, :].rearrange("p (c i) j -> p c j i", i=4)
+            src = raw[a][u][:, :, lo:hi].rearrange("p j (c i) -> p c j i", i=4)
+            if on_vector:
+                nc.vector.tensor_copy(out=dst, in_=src)
+            else:
+                nc.scalar.activation(out=dst, in_=src, func=ACT.Copy)
+
+        def quantize(a, u):
+            cols = slice(u * UNIT, (u + 1) * UNIT)
+            nc.vector.quantize_mx(
+                out=codes[a][:, cols].bitcast(FP8X4),
+                scales=scales[4 * a:P, cols],
+                in_=grouped[a][:, cols, :].rearrange("p t j -> p (t j)"),
+            )
+
+        def gather(dst, window, lo, hi):
+            nc.vector.tensor_copy(dst[:, lo:hi], window[:].indirect(offsets[:, lo // 16:hi // 16]))
+
+        for a in range(PASSES):
+            for u in range(UNITS):
+                if a == 0:
+                    cast(a, u, 0, 96, False)
+                    cast(a, u, 96, UNIT, True)
+                else:
+                    cast(a, u, 0, UNIT, False)
+                quantize(a, u)
+            if a < PASSES - 1:
+                for lo in range(0, S, 512):
+                    gather(slot_codes[a], codes[a], lo, lo + 512)
+
+        for lo in range(0, S, 512):
+            gather(slot_scales, scales, lo, lo + 512)
+            for a in range(1, PASSES):
+                queue = nc.scalar if a == 2 else nc.sync
+                queue.dma_start(
+                    out=moved_scales[0:SHIFT_ROWS, a - 1, lo:lo + 512].bitcast(I32),
+                    in_=slot_scales[4 * a:4 * a + SHIFT_ROWS, lo:lo + 512].bitcast(I32),
+                )
+
+        def multiply(e, m, a):
+            cols = slice(e * C + m * U, e * C + (m + 1) * U)
+            plane = slot_scales[:, cols] if a == 0 else moved_scales[:, a - 1, cols]
+            nc.tensor.matmul_mx(
+                out=acc[e][:, m, :],
+                lhsT=w_codes[:, e * PASSES + a, :].bitcast(FP4X4),
+                lhsT_scale=w_planes[:, e * PASSES + a, :],
+                rhs=slot_codes[a][:, cols].bitcast(FP8X4),
+                rhs_scale=plane,
+                start=(a == 0),
+                stop=(a == PASSES - 1),
+            )
+
+        out_by_rank = out.rearrange("n (m x) -> n m x", m=R)
+        last = PASSES - 1
+        stored = 0
+        for e in range(E):
+            gather(slot_codes[last], codes[last], e * C, (e + 1) * C)
+            for m in range(R):
+                for a in range(PASSES):
+                    multiply(e, m, a)
+            cols = slice(e * U, (e + 1) * U)
+            nc.scalar.activation(out=result[:, :, cols], in_=acc[e][:], func=ACT.Silu, bias=bias[:, e:e + 1])
+            if e % 2 == 1 or e == E - 2:
+                cols = slice(stored * U, (e + 1) * U)
+                nc.sync.dma_start(out=out_by_rank[:, :, cols], in_=result[:, :, cols])
+                stored = e + 1

@@ -24,6 +24,7 @@ UNIT = 256
 UNITS = T // UNIT
 U = C // R
 SHIFT_ROWS = 112
+SCALE_PIECES = [(0, 2), (2, 5), (5, 8)]
 
 
 def tile_moe_eps_lin_silu_kernel(tc, xT, w_words, w_scales, b, offs, out):
@@ -58,9 +59,8 @@ def tile_moe_eps_lin_silu_kernel(tc, xT, w_words, w_scales, b, offs, out):
             rows = xT[a * K_PASS:(a + 1) * K_PASS, :].rearrange("(p j) t -> p j t", j=PACK)
             for u in range(UNITS):
                 nc.sync.dma_start(out=raw[a][u][:], in_=rows[:, :, u * UNIT:(u + 1) * UNIT])
-            if a == 0:
-                nc.sync.dma_start(offsets[:], offs)
-                nc.sync.dma_start(out=bias[:], in_=b)
+                if a == 0 and u == 2:
+                    nc.sync.dma_start(offsets[:], offs)
         scale_rows = w_scales.rearrange("e a q n -> q (e a) n").bitcast(I32)
         for quad in range(4):
             nc.sync.dma_start(out=w_planes[32 * quad:32 * quad + 4].bitcast(I32), in_=scale_rows[4 * quad:4 * quad + 4])
@@ -68,6 +68,8 @@ def tile_moe_eps_lin_silu_kernel(tc, xT, w_words, w_scales, b, offs, out):
         for pair in range(E // 2):
             mats = slice(2 * pair * PASSES, 2 * (pair + 1) * PASSES)
             nc.sync.dma_start(out=w_codes[:, mats, :].bitcast(I32), in_=word_rows[:, mats, :])
+
+        nc.sync.dma_start(out=bias[:], in_=b)
 
         def cast(a, u, lo, hi, on_vector):
             dst = grouped[a][:, u * UNIT + lo:u * UNIT + hi, :].rearrange("p (c i) j -> p c j i", i=4)
@@ -100,15 +102,6 @@ def tile_moe_eps_lin_silu_kernel(tc, xT, w_words, w_scales, b, offs, out):
                 for lo in range(0, S, 512):
                     gather(slot_codes[a], codes[a], lo, lo + 512)
 
-        for lo in range(0, S, 512):
-            gather(slot_scales, scales, lo, lo + 512)
-            for a in range(1, PASSES):
-                queue = nc.scalar if a == 2 else nc.sync
-                queue.dma_start(
-                    out=moved_scales[0:SHIFT_ROWS, a - 1, lo:lo + 512].bitcast(I32),
-                    in_=slot_scales[4 * a:4 * a + SHIFT_ROWS, lo:lo + 512].bitcast(I32),
-                )
-
         def multiply(e, m, a):
             cols = slice(e * C + m * U, e * C + (m + 1) * U)
             plane = slot_scales[:, cols] if a == 0 else moved_scales[:, a - 1, cols]
@@ -122,14 +115,27 @@ def tile_moe_eps_lin_silu_kernel(tc, xT, w_words, w_scales, b, offs, out):
                 stop=(a == PASSES - 1),
             )
 
-        out_by_rank = out.rearrange("n (m x) -> n m x", m=R)
         last = PASSES - 1
+        for piece, (e_lo, e_hi) in enumerate(SCALE_PIECES):
+            lo, hi = e_lo * C, e_hi * C
+            gather(slot_scales, scales, lo, hi)
+            for a in range(1, PASSES):
+                queue = nc.sync
+                queue.dma_start(
+                    out=moved_scales[0:SHIFT_ROWS, a - 1, lo:hi].bitcast(I32),
+                    in_=slot_scales[4 * a:4 * a + SHIFT_ROWS, lo:hi].bitcast(I32),
+                )
+            for e in range(e_lo, e_hi):
+                for a in range(last):
+                    multiply(e, 0, a)
+
+        out_by_rank = out.rearrange("n (m x) -> n m x", m=R)
         stored = 0
         for e in range(E):
             gather(slot_codes[last], codes[last], e * C, (e + 1) * C)
-            for m in range(R):
-                for a in range(PASSES):
-                    multiply(e, m, a)
+            multiply(e, 0, last)
+            for a in range(PASSES):
+                multiply(e, 1, a)
             cols = slice(e * U, (e + 1) * U)
             nc.scalar.activation(out=result[:, :, cols], in_=acc[e][:], func=ACT.Silu, bias=bias[:, e:e + 1])
             if e % 2 == 1 or e == E - 2:

@@ -24,7 +24,8 @@ UNIT = 256
 UNITS = T // UNIT
 U = C // R
 SHIFT_ROWS = 112
-SCALE_PIECES = [(0, 2), (2, 5), (5, 8)]
+BANKS = 8
+WORD_PIECES = [(0, 768), (768, 1408), (1408, 2048)]
 
 
 def tile_moe_eps_lin_silu_kernel(tc, xT, w_words, w_scales, b, offs, out):
@@ -47,7 +48,7 @@ def tile_moe_eps_lin_silu_kernel(tc, xT, w_words, w_scales, b, offs, out):
         result = keep.tile([P, R, E * U], F32, name="result")
         warm_in = keep.tile([P, 1], F32, name="warm_in")
         warm_out = keep.tile([P, 1], F32, name="warm_out")
-        acc = [psum.tile([P, R, U], F32, name="acc%d" % e) for e in range(E)]
+        banks = [psum.tile([P, C], F32, name="bank%d" % i) for i in range(BANKS)]
 
         nc.vector.memset(warm_in[:], 0.0)
         nc.scalar.activation(out=warm_out[:], in_=warm_in[:], func=ACT.Silu)
@@ -79,8 +80,8 @@ def tile_moe_eps_lin_silu_kernel(tc, xT, w_words, w_scales, b, offs, out):
             else:
                 nc.scalar.activation(out=dst, in_=src, func=ACT.Copy)
 
-        def quantize(a, u):
-            cols = slice(u * UNIT, (u + 1) * UNIT)
+        def quantize(a, u_lo, u_hi):
+            cols = slice(u_lo * UNIT, u_hi * UNIT)
             nc.vector.quantize_mx(
                 out=codes[a][:, cols].bitcast(FP8X4),
                 scales=scales[4 * a:P, cols],
@@ -92,21 +93,24 @@ def tile_moe_eps_lin_silu_kernel(tc, xT, w_words, w_scales, b, offs, out):
 
         for a in range(PASSES):
             for u in range(UNITS):
-                if a == 0:
+                if a == 0 or (a == PASSES - 1 and u == UNITS - 1):
                     cast(a, u, 0, 96, False)
                     cast(a, u, 96, UNIT, True)
                 else:
                     cast(a, u, 0, UNIT, False)
-                quantize(a, u)
+                if u % 2 == 1:
+                    quantize(a, u - 1, u + 1)
+                elif u == UNITS - 1:
+                    quantize(a, u, u + 1)
             if a < PASSES - 1:
-                for lo in range(0, S, 512):
-                    gather(slot_codes[a], codes[a], lo, lo + 512)
+                for lo, hi in WORD_PIECES:
+                    gather(slot_codes[a], codes[a], lo, hi)
 
         def multiply(e, m, a):
             cols = slice(e * C + m * U, e * C + (m + 1) * U)
             plane = slot_scales[:, cols] if a == 0 else moved_scales[:, a - 1, cols]
             nc.tensor.matmul_mx(
-                out=acc[e][:, m, :],
+                out=banks[(R * e + m) % BANKS][:, 0:U],
                 lhsT=w_codes[:, e * PASSES + a, :].bitcast(FP4X4),
                 lhsT_scale=w_planes[:, e * PASSES + a, :],
                 rhs=slot_codes[a][:, cols].bitcast(FP8X4),
@@ -116,29 +120,62 @@ def tile_moe_eps_lin_silu_kernel(tc, xT, w_words, w_scales, b, offs, out):
             )
 
         last = PASSES - 1
-        for piece, (e_lo, e_hi) in enumerate(SCALE_PIECES):
+        out_by_rank = out.rearrange("n (m x) -> n m x", m=R)
+
+        def scale_piece(e_lo, e_hi):
             lo, hi = e_lo * C, e_hi * C
             gather(slot_scales, scales, lo, hi)
             for a in range(1, PASSES):
-                queue = nc.sync
-                queue.dma_start(
+                nc.sync.dma_start(
                     out=moved_scales[0:SHIFT_ROWS, a - 1, lo:hi].bitcast(I32),
                     in_=slot_scales[4 * a:4 * a + SHIFT_ROWS, lo:hi].bitcast(I32),
                 )
-            for e in range(e_lo, e_hi):
-                for a in range(last):
-                    multiply(e, 0, a)
 
-        out_by_rank = out.rearrange("n (m x) -> n m x", m=R)
-        stored = 0
-        for e in range(E):
-            gather(slot_codes[last], codes[last], e * C, (e + 1) * C)
-            multiply(e, 0, last)
-            for a in range(PASSES):
-                multiply(e, 1, a)
-            cols = slice(e * U, (e + 1) * U)
-            nc.scalar.activation(out=result[:, :, cols], in_=acc[e][:], func=ACT.Silu, bias=bias[:, e:e + 1])
-            if e % 2 == 1 or e == E - 2:
-                cols = slice(stored * U, (e + 1) * U)
-                nc.sync.dma_start(out=out_by_rank[:, :, cols], in_=result[:, :, cols])
-                stored = e + 1
+        def early(experts, passes):
+            for a in passes:
+                for e in experts:
+                    for m in range(R):
+                        multiply(e, m, a)
+
+        def finish(e_lo, e_hi):
+            gather(slot_codes[last], codes[last], e_lo * C, e_hi * C)
+            for e in range(e_lo, e_hi):
+                for m in range(R):
+                    multiply(e, m, last)
+                    nc.scalar.activation(
+                        out=result[:, m, e * U:(e + 1) * U],
+                        in_=banks[(R * e + m) % BANKS][:, 0:U],
+                        func=ACT.Silu,
+                        bias=bias[:, e:e + 1],
+                    )
+            cols = slice(e_lo * U, e_hi * U)
+            nc.sync.dma_start(out=out_by_rank[:, :, cols], in_=result[:, :, cols])
+
+        scale_piece(0, 2)
+        early((0, 1), (0,))
+        for i in range(4):
+            e = i % 2
+            cols = slice(e * C, (e + 1) * C)
+            nc.tensor.matmul_mx(
+                out=banks[4 + i][:],
+                lhsT=w_codes[:, e * PASSES, :].bitcast(FP4X4),
+                lhsT_scale=w_planes[:, e * PASSES, :],
+                rhs=slot_codes[0][:, cols].bitcast(FP8X4),
+                rhs_scale=slot_scales[:, cols],
+                start=True,
+                stop=True,
+            )
+        scale_piece(2, 5)
+        early((2, 3), (0,))
+        early((0, 1), (1, 2))
+        early((2, 3), (1, 2))
+        scale_piece(5, 8)
+        finish(0, 2)
+        early((4,), (0, 1, 2))
+        early((5,), (0, 1))
+        finish(2, 4)
+        early((5,), (2,))
+        early((6, 7), (0, 1, 2))
+        finish(4, 6)
+        finish(6, 7)
+        finish(7, 8)

@@ -20,8 +20,16 @@ P = 128
 PACK = 4
 K_PASS = P * PACK
 PASSES = K // K_PASS
-UNIT = 256
-UNITS = T // UNIT
+FIRST = (
+    [(0, 512), (512, 1024), (1024, 1280)],
+    [(0, 192), (512, 704), (1024, 1120)],
+    [(192, 512), (704, 1024), (1120, 1280)],
+    [(0, 512), (512, 1024), (1024, 1280)],
+)
+THIRDS = [(0, 512), (512, 1024), (1024, 1280)]
+MIDDLE = (THIRDS, THIRDS, [], THIRDS)
+LAST = (THIRDS, [(0, 512), (512, 1024), (1024, 1152)], [(1152, 1280)], THIRDS)
+PLAN = [FIRST, MIDDLE, MIDDLE, LAST]
 U = C // R
 SHIFT_ROWS = 112
 BANKS = 8
@@ -36,7 +44,8 @@ def tile_moe_eps_lin_silu_kernel(tc, xT, w_words, w_scales, b, offs, out):
 
         offsets = keep.tile([P, S // 16], U16, name="offsets")
         bias = keep.tile([P, E], F32, name="bias")
-        raw = [[keep.tile([P, PACK, UNIT], F32, name="raw%d_%d" % (a, u)) for u in range(UNITS)] for a in range(PASSES)]
+        raw = [[keep.tile([P, PACK, hi - lo], F32, name="raw%d_%d" % (a, lo)) for lo, hi in PLAN[a][0]] for a in range(PASSES)]
+        w_rows = keep.tile([16, E * PASSES, N // 4], I32, name="w_rows")
         grouped = [keep.tile([P, T, PACK], BF16, name="grouped%d" % a, align_bytes=64) for a in range(PASSES)]
         codes = [keep.tile([P, T], U32, name="codes%d" % a, align_bytes=64) for a in range(PASSES)]
         scales = keep.tile([P, T], U8, name="scales", align_bytes=64)
@@ -56,32 +65,34 @@ def tile_moe_eps_lin_silu_kernel(tc, xT, w_words, w_scales, b, offs, out):
         nc.vector.memset(w_planes[:].bitcast(I32), 0)
         nc.vector.memset(moved_scales[:].bitcast(I32), 0)
 
+        nc.scalar.dma_start(out=bias[:], in_=b)
         for a in range(PASSES):
             rows = xT[a * K_PASS:(a + 1) * K_PASS, :].rearrange("(p j) t -> p j t", j=PACK)
-            for u in range(UNITS):
-                nc.sync.dma_start(out=raw[a][u][:], in_=rows[:, :, u * UNIT:(u + 1) * UNIT])
-                if a == 0 and u == 2:
-                    nc.sync.dma_start(offsets[:], offs)
-        scale_rows = w_scales.rearrange("e a q n -> q (e a) n").bitcast(I32)
+            for u, (lo, hi) in enumerate(PLAN[a][0]):
+                nc.sync.dma_start(out=raw[a][u][:], in_=rows[:, :, lo:hi])
+            if a == 0:
+                nc.sync.dma_start(offsets[:], offs)
+            if a == 1:
+                nc.sync.dma_start(out=w_rows[:], in_=w_scales.rearrange("e a q n -> q (e a) n").bitcast(I32))
         for quad in range(4):
-            nc.sync.dma_start(out=w_planes[32 * quad:32 * quad + 4].bitcast(I32), in_=scale_rows[4 * quad:4 * quad + 4])
+            nc.sync.dma_start(out=w_planes[32 * quad:32 * quad + 4].bitcast(I32), in_=w_rows[4 * quad:4 * quad + 4])
         word_rows = w_words.rearrange("e a p c -> p (e a) c").bitcast(I32)
         for pair in range(E // 2):
             mats = slice(2 * pair * PASSES, 2 * (pair + 1) * PASSES)
             nc.sync.dma_start(out=w_codes[:, mats, :].bitcast(I32), in_=word_rows[:, mats, :])
 
-        nc.sync.dma_start(out=bias[:], in_=b)
-
-        def cast(a, u, lo, hi, on_vector):
-            dst = grouped[a][:, u * UNIT + lo:u * UNIT + hi, :].rearrange("p (c i) j -> p c j i", i=4)
-            src = raw[a][u][:, :, lo:hi].rearrange("p j (c i) -> p c j i", i=4)
+        def cast(a, lo, hi, on_vector):
+            u = max(i for i, load in enumerate(PLAN[a][0]) if load[0] <= lo)
+            first = PLAN[a][0][u][0]
+            dst = grouped[a][:, lo:hi, :].rearrange("p (c i) j -> p c j i", i=4)
+            src = raw[a][u][:, :, lo - first:hi - first].rearrange("p j (c i) -> p c j i", i=4)
             if on_vector:
                 nc.vector.tensor_copy(out=dst, in_=src)
             else:
                 nc.scalar.activation(out=dst, in_=src, func=ACT.Copy)
 
-        def quantize(a, u_lo, u_hi):
-            cols = slice(u_lo * UNIT, u_hi * UNIT)
+        def quantize(a, lo, hi):
+            cols = slice(lo, hi)
             nc.vector.quantize_mx(
                 out=codes[a][:, cols].bitcast(FP8X4),
                 scales=scales[4 * a:P, cols],
@@ -92,16 +103,12 @@ def tile_moe_eps_lin_silu_kernel(tc, xT, w_words, w_scales, b, offs, out):
             nc.vector.tensor_copy(dst[:, lo:hi], window[:].indirect(offsets[:, lo // 16:hi // 16]))
 
         for a in range(PASSES):
-            for u in range(UNITS):
-                if a == 0 or (a == PASSES - 1 and u == UNITS - 1):
-                    cast(a, u, 0, 96, False)
-                    cast(a, u, 96, UNIT, True)
-                else:
-                    cast(a, u, 0, UNIT, False)
-                if u % 2 == 1:
-                    quantize(a, u - 1, u + 1)
-                elif u == UNITS - 1:
-                    quantize(a, u, u + 1)
+            for lo, hi in PLAN[a][1]:
+                cast(a, lo, hi, False)
+            for lo, hi in PLAN[a][2]:
+                cast(a, lo, hi, True)
+            for lo, hi in PLAN[a][3]:
+                quantize(a, lo, hi)
             if a < PASSES - 1:
                 for lo, hi in WORD_PIECES:
                     gather(slot_codes[a], codes[a], lo, hi)
@@ -126,7 +133,8 @@ def tile_moe_eps_lin_silu_kernel(tc, xT, w_words, w_scales, b, offs, out):
             lo, hi = e_lo * C, e_hi * C
             gather(slot_scales, scales, lo, hi)
             for a in range(1, PASSES):
-                nc.sync.dma_start(
+                queue = nc.sync if a == last else nc.scalar
+                queue.dma_start(
                     out=moved_scales[0:SHIFT_ROWS, a - 1, lo:hi].bitcast(I32),
                     in_=slot_scales[4 * a:4 * a + SHIFT_ROWS, lo:hi].bitcast(I32),
                 )
@@ -153,18 +161,6 @@ def tile_moe_eps_lin_silu_kernel(tc, xT, w_words, w_scales, b, offs, out):
 
         scale_piece(0, 2)
         early((0, 1), (0,))
-        for i in range(4):
-            e = i % 2
-            cols = slice(e * C, (e + 1) * C)
-            nc.tensor.matmul_mx(
-                out=banks[4 + i][:],
-                lhsT=w_codes[:, e * PASSES, :].bitcast(FP4X4),
-                lhsT_scale=w_planes[:, e * PASSES, :],
-                rhs=slot_codes[0][:, cols].bitcast(FP8X4),
-                rhs_scale=slot_scales[:, cols],
-                start=True,
-                stop=True,
-            )
         scale_piece(2, 5)
         early((2, 3), (0,))
         early((0, 1), (1, 2))

@@ -20,20 +20,16 @@ P = 128
 PACK = 4
 K_PASS = P * PACK
 PASSES = K // K_PASS
-FIRST = (
-    [(0, 512), (512, 1024), (1024, 1280)],
-    [(0, 192), (512, 704), (1024, 1120)],
-    [(192, 512), (704, 1024), (1120, 1280)],
-    [(0, 512), (512, 1024), (1024, 1280)],
-)
-THIRDS = [(0, 512), (512, 1024), (1024, 1280)]
-MIDDLE = (THIRDS, THIRDS, [], THIRDS)
-LAST = (THIRDS, [(0, 512), (512, 1024), (1024, 1152)], [(1152, 1280)], THIRDS)
-PLAN = [FIRST, MIDDLE, MIDDLE, LAST]
+LAST = PASSES - 1
+RANK_T = T // R
 U = C // R
+PAIR = 2 * C
 SHIFT_ROWS = 112
 BANKS = 8
-WORD_PIECES = [(0, 768), (768, 1408), (1408, 2048)]
+WORD_PIECES = [(0, 768), (768, 1536)]
+SHARED = ([(0, 256)], [(256, 640)], [(256, 512), (512, 640), (0, 256)])
+SCALAR_ONLY = ([(0, 512), (512, 640)], [], [(0, 512), (512, 640)])
+SPLIT_PASSES = 2
 
 
 def tile_moe_eps_lin_silu_kernel(tc, xT, w_words, w_scales, b, offs, out):
@@ -44,10 +40,11 @@ def tile_moe_eps_lin_silu_kernel(tc, xT, w_words, w_scales, b, offs, out):
 
         offsets = keep.tile([P, S // 16], U16, name="offsets")
         bias = keep.tile([P, E], F32, name="bias")
-        raw = [[keep.tile([P, PACK, hi - lo], F32, name="raw%d_%d" % (a, lo)) for lo, hi in PLAN[a][0]] for a in range(PASSES)]
-        w_rows = keep.tile([16, E * PASSES, N // 4], I32, name="w_rows")
+        raw = [[keep.tile([P, PACK, RANK_T], F32, name="raw%d_%d" % (a, m)) for m in range(R)] for a in range(PASSES)]
         grouped = [keep.tile([P, T, PACK], BF16, name="grouped%d" % a, align_bytes=64) for a in range(PASSES)]
-        codes = [keep.tile([P, T], U32, name="codes%d" % a, align_bytes=64) for a in range(PASSES)]
+        codes = [keep.tile([P, T], U32, name="codes%d" % a, align_bytes=64)[:] for a in range(SPLIT_PASSES)]
+        late_codes = keep.tile([P, 2 * T], U32, name="late_codes", align_bytes=64)
+        codes = codes + [late_codes[:, 0:T], late_codes[:, T:2 * T]]
         scales = keep.tile([P, T], U8, name="scales", align_bytes=64)
         slot_codes = [keep.tile([P, S], U32, name="slot_codes%d" % a, align_bytes=64) for a in range(PASSES)]
         slot_scales = keep.tile([P, S], U8, name="slot_scales", align_bytes=64)
@@ -57,7 +54,7 @@ def tile_moe_eps_lin_silu_kernel(tc, xT, w_words, w_scales, b, offs, out):
         result = keep.tile([P, R, E * U], F32, name="result")
         warm_in = keep.tile([P, 1], F32, name="warm_in")
         warm_out = keep.tile([P, 1], F32, name="warm_out")
-        banks = [psum.tile([P, C], F32, name="bank%d" % i) for i in range(BANKS)]
+        banks = [psum.tile([P, U], F32, name="bank%d" % i) for i in range(BANKS)]
 
         nc.vector.memset(warm_in[:], 0.0)
         nc.scalar.activation(out=warm_out[:], in_=warm_in[:], func=ACT.Silu)
@@ -68,31 +65,28 @@ def tile_moe_eps_lin_silu_kernel(tc, xT, w_words, w_scales, b, offs, out):
         nc.scalar.dma_start(out=bias[:], in_=b)
         for a in range(PASSES):
             rows = xT[a * K_PASS:(a + 1) * K_PASS, :].rearrange("(p j) t -> p j t", j=PACK)
-            for u, (lo, hi) in enumerate(PLAN[a][0]):
-                nc.sync.dma_start(out=raw[a][u][:], in_=rows[:, :, lo:hi])
-            if a == 0:
-                nc.sync.dma_start(offsets[:], offs)
-            if a == 1:
-                nc.sync.dma_start(out=w_rows[:], in_=w_scales.rearrange("e a q n -> q (e a) n").bitcast(I32))
+            for m in range(R):
+                nc.sync.dma_start(out=raw[a][m][:], in_=rows[:, :, m * RANK_T:(m + 1) * RANK_T])
+                if a == 0 and m == 0:
+                    nc.sync.dma_start(offsets[:], offs)
+        scale_rows = w_scales.rearrange("e a q n -> q (e a) n").bitcast(I32)
         for quad in range(4):
-            nc.sync.dma_start(out=w_planes[32 * quad:32 * quad + 4].bitcast(I32), in_=w_rows[4 * quad:4 * quad + 4])
+            nc.sync.dma_start(out=w_planes[32 * quad:32 * quad + 4].bitcast(I32), in_=scale_rows[4 * quad:4 * quad + 4])
         word_rows = w_words.rearrange("e a p c -> p (e a) c").bitcast(I32)
         for pair in range(E // 2):
             mats = slice(2 * pair * PASSES, 2 * (pair + 1) * PASSES)
             nc.sync.dma_start(out=w_codes[:, mats, :].bitcast(I32), in_=word_rows[:, mats, :])
 
-        def cast(a, lo, hi, on_vector):
-            u = max(i for i, load in enumerate(PLAN[a][0]) if load[0] <= lo)
-            first = PLAN[a][0][u][0]
-            dst = grouped[a][:, lo:hi, :].rearrange("p (c i) j -> p c j i", i=4)
-            src = raw[a][u][:, :, lo - first:hi - first].rearrange("p j (c i) -> p c j i", i=4)
+        def cast(a, m, lo, hi, on_vector):
+            dst = grouped[a][:, m * RANK_T + lo:m * RANK_T + hi, :].rearrange("p (c i) j -> p c j i", i=4)
+            src = raw[a][m][:, :, lo:hi].rearrange("p j (c i) -> p c j i", i=4)
             if on_vector:
                 nc.vector.tensor_copy(out=dst, in_=src)
             else:
                 nc.scalar.activation(out=dst, in_=src, func=ACT.Copy)
 
-        def quantize(a, lo, hi):
-            cols = slice(lo, hi)
+        def quantize(a, m, lo, hi):
+            cols = slice(m * RANK_T + lo, m * RANK_T + hi)
             nc.vector.quantize_mx(
                 out=codes[a][:, cols].bitcast(FP8X4),
                 scales=scales[4 * a:P, cols],
@@ -100,16 +94,24 @@ def tile_moe_eps_lin_silu_kernel(tc, xT, w_words, w_scales, b, offs, out):
             )
 
         def gather(dst, window, lo, hi):
-            nc.vector.tensor_copy(dst[:, lo:hi], window[:].indirect(offsets[:, lo // 16:hi // 16]))
+            nc.vector.tensor_copy(dst[:, lo:hi], window.indirect(offsets[:, lo // 16:hi // 16]))
 
         for a in range(PASSES):
-            for lo, hi in PLAN[a][1]:
-                cast(a, lo, hi, False)
-            for lo, hi in PLAN[a][2]:
-                cast(a, lo, hi, True)
-            for lo, hi in PLAN[a][3]:
-                quantize(a, lo, hi)
-            if a < PASSES - 1:
+            on_scalar, on_vector, quantised = SHARED if a == 0 else SCALAR_ONLY
+            for m in range(R):
+                for lo, hi in on_scalar:
+                    cast(a, m, lo, hi, False)
+                for lo, hi in on_vector:
+                    cast(a, m, lo, hi, True)
+                for lo, hi in quantised:
+                    quantize(a, m, lo, hi)
+                if a < SPLIT_PASSES:
+                    for first in range(0, S, PAIR):
+                        if m == 0:
+                            gather(slot_codes[a], codes[a][:, 0:RANK_T], first, first + U)
+                        else:
+                            gather(slot_codes[a], codes[a], first + U, first + PAIR)
+            if SPLIT_PASSES <= a < LAST:
                 for lo, hi in WORD_PIECES:
                     gather(slot_codes[a], codes[a], lo, hi)
 
@@ -117,24 +119,23 @@ def tile_moe_eps_lin_silu_kernel(tc, xT, w_words, w_scales, b, offs, out):
             cols = slice(e * C + m * U, e * C + (m + 1) * U)
             plane = slot_scales[:, cols] if a == 0 else moved_scales[:, a - 1, cols]
             nc.tensor.matmul_mx(
-                out=banks[(R * e + m) % BANKS][:, 0:U],
+                out=banks[(R * e + m) % BANKS][:],
                 lhsT=w_codes[:, e * PASSES + a, :].bitcast(FP4X4),
                 lhsT_scale=w_planes[:, e * PASSES + a, :],
                 rhs=slot_codes[a][:, cols].bitcast(FP8X4),
                 rhs_scale=plane,
                 start=(a == 0),
-                stop=(a == PASSES - 1),
+                stop=(a == LAST),
             )
 
-        last = PASSES - 1
         out_by_rank = out.rearrange("n (m x) -> n m x", m=R)
 
         def scale_piece(e_lo, e_hi):
             lo, hi = e_lo * C, e_hi * C
-            gather(slot_scales, scales, lo, hi)
+            for first in range(lo, hi, PAIR):
+                gather(slot_scales, scales[:], first, first + PAIR)
             for a in range(1, PASSES):
-                queue = nc.sync if a == last else nc.scalar
-                queue.dma_start(
+                nc.sync.dma_start(
                     out=moved_scales[0:SHIFT_ROWS, a - 1, lo:hi].bitcast(I32),
                     in_=slot_scales[4 * a:4 * a + SHIFT_ROWS, lo:hi].bitcast(I32),
                 )
@@ -146,32 +147,28 @@ def tile_moe_eps_lin_silu_kernel(tc, xT, w_words, w_scales, b, offs, out):
                         multiply(e, m, a)
 
         def finish(e_lo, e_hi):
-            gather(slot_codes[last], codes[last], e_lo * C, e_hi * C)
+            gather(slot_codes[LAST], codes[LAST], e_lo * C, e_hi * C)
             for e in range(e_lo, e_hi):
                 for m in range(R):
-                    multiply(e, m, last)
+                    multiply(e, m, LAST)
                     nc.scalar.activation(
                         out=result[:, m, e * U:(e + 1) * U],
-                        in_=banks[(R * e + m) % BANKS][:, 0:U],
+                        in_=banks[(R * e + m) % BANKS][:],
                         func=ACT.Silu,
                         bias=bias[:, e:e + 1],
                     )
             cols = slice(e_lo * U, e_hi * U)
             nc.sync.dma_start(out=out_by_rank[:, :, cols], in_=result[:, :, cols])
 
-        scale_piece(0, 2)
-        early((0, 1), (0,))
-        scale_piece(2, 5)
-        early((2, 3), (0,))
-        early((0, 1), (1, 2))
-        early((2, 3), (1, 2))
-        scale_piece(5, 8)
+        scale_piece(0, 4)
+        early(range(0, 4), (0,))
+        scale_piece(4, 8)
+        early(range(0, 4), (1, 2))
         finish(0, 2)
-        early((4,), (0, 1, 2))
-        early((5,), (0, 1))
         finish(2, 4)
-        early((5,), (2,))
-        early((6, 7), (0, 1, 2))
+        early(range(4, 6), (0, 1, 2))
         finish(4, 6)
+        gather(slot_codes[LAST - 1], late_codes[:], 6 * C, S)
+        early(range(6, 8), (0, 1, 2))
         finish(6, 7)
         finish(7, 8)

@@ -29,6 +29,7 @@ BANKS = 8
 WORD_PIECES = [(0, 768), (768, 1536)]
 SHARED = ([(0, 256)], [(256, 640)], [(256, 512), (512, 640), (0, 256)])
 SCALAR_ONLY = ([(0, 512), (512, 640)], [], [(0, 512), (512, 640)])
+TAIL_SHARED = ([(0, 256), (256, 384)], [(384, 640)], [(384, 640), (0, 256), (256, 384)])
 SPLIT_PASSES = 2
 
 
@@ -51,6 +52,7 @@ def tile_moe_eps_lin_silu_kernel(tc, xT, w_words, w_scales, b, offs, out):
         moved_scales = keep.tile([P, PASSES - 1, S], U8, name="moved_scales", align_bytes=64)
         w_codes = keep.tile([P, E * PASSES, 2 * N], U8, name="w_codes", align_bytes=64)
         w_planes = keep.tile([P, E * PASSES, N], U8, name="w_planes", align_bytes=64)
+        w_rows = keep.tile([16, E * PASSES, N // 4], I32, name="w_rows")
         result = keep.tile([P, R, E * U], F32, name="result")
         warm_in = keep.tile([P, 1], F32, name="warm_in")
         warm_out = keep.tile([P, 1], F32, name="warm_out")
@@ -69,13 +71,13 @@ def tile_moe_eps_lin_silu_kernel(tc, xT, w_words, w_scales, b, offs, out):
                 nc.sync.dma_start(out=raw[a][m][:], in_=rows[:, :, m * RANK_T:(m + 1) * RANK_T])
                 if a == 0 and m == 0:
                     nc.sync.dma_start(offsets[:], offs)
-        scale_rows = w_scales.rearrange("e a q n -> q (e a) n").bitcast(I32)
-        for quad in range(4):
-            nc.sync.dma_start(out=w_planes[32 * quad:32 * quad + 4].bitcast(I32), in_=scale_rows[4 * quad:4 * quad + 4])
+        nc.sync.dma_start(out=w_rows[:], in_=w_scales.rearrange("e a q n -> q (e a) n").bitcast(I32))
         word_rows = w_words.rearrange("e a p c -> p (e a) c").bitcast(I32)
         for pair in range(E // 2):
             mats = slice(2 * pair * PASSES, 2 * (pair + 1) * PASSES)
             nc.sync.dma_start(out=w_codes[:, mats, :].bitcast(I32), in_=word_rows[:, mats, :])
+        for quad in range(4):
+            nc.sync.dma_start(out=w_planes[32 * quad:32 * quad + 4].bitcast(I32), in_=w_rows[4 * quad:4 * quad + 4])
 
         def cast(a, m, lo, hi, on_vector):
             dst = grouped[a][:, m * RANK_T + lo:m * RANK_T + hi, :].rearrange("p (c i) j -> p c j i", i=4)
@@ -97,8 +99,8 @@ def tile_moe_eps_lin_silu_kernel(tc, xT, w_words, w_scales, b, offs, out):
             nc.vector.tensor_copy(dst[:, lo:hi], window.indirect(offsets[:, lo // 16:hi // 16]))
 
         for a in range(PASSES):
-            on_scalar, on_vector, quantised = SHARED if a == 0 else SCALAR_ONLY
             for m in range(R):
+                on_scalar, on_vector, quantised = SHARED if a == 0 else TAIL_SHARED if a >= SPLIT_PASSES and m == R - 1 else SCALAR_ONLY
                 for lo, hi in on_scalar:
                     cast(a, m, lo, hi, False)
                 for lo, hi in on_vector:
@@ -157,8 +159,11 @@ def tile_moe_eps_lin_silu_kernel(tc, xT, w_words, w_scales, b, offs, out):
                         func=ACT.Silu,
                         bias=bias[:, e:e + 1],
                     )
+                    if e == E - 1:
+                        nc.sync.dma_start(out=out_by_rank[:, m, e * U:], in_=result[:, m, e * U:])
             cols = slice(e_lo * U, e_hi * U)
-            nc.sync.dma_start(out=out_by_rank[:, :, cols], in_=result[:, :, cols])
+            if e_hi < E:
+                nc.sync.dma_start(out=out_by_rank[:, :, cols], in_=result[:, :, cols])
 
         scale_piece(0, 4)
         early(range(0, 4), (0,))

@@ -24,13 +24,15 @@ LAST = PASSES - 1
 RANK_T = T // R
 U = C // R
 PAIR = 2 * C
-SHIFT_ROWS = 112
+LIST_GROUP = 16
+QUADRANT = 32
+SCALE_ROWS = 4
+MOVED_ROWS = 112
 BANKS = 8
-WORD_PIECES = [(0, 768), (768, 1536)]
-SHARED = ([(0, 256)], [(256, 640)], [(256, 512), (512, 640), (0, 256)])
-SCALAR_ONLY = ([(0, 512), (512, 640)], [], [(0, 512), (512, 640)])
-TAIL_SHARED = ([(0, 256), (256, 384)], [(384, 640)], [(384, 640), (0, 256), (256, 384)])
-SPLIT_PASSES = 2
+
+FIRST_PASS = ([(0, 256)], [(256, 640)], [(256, 512), (512, 640), (0, 256)])
+SCALAR_ALONE = ([(0, 512), (512, 640)], [], [(0, 512), (512, 640)])
+LAST_LOAD = ([(0, 256), (256, 384)], [(384, 640)], [(384, 640), (0, 256), (256, 384)])
 
 
 def tile_moe_eps_lin_silu_kernel(tc, xT, w_words, w_scales, b, offs, out):
@@ -39,11 +41,11 @@ def tile_moe_eps_lin_silu_kernel(tc, xT, w_words, w_scales, b, offs, out):
         keep = ctx.enter_context(tc.tile_pool(name="keep", bufs=1))
         psum = ctx.enter_context(tc.psum_pool(name="psum", bufs=1))
 
-        offsets = keep.tile([P, S // 16], U16, name="offsets")
+        offsets = keep.tile([P, S // LIST_GROUP], U16, name="offsets")
         bias = keep.tile([P, E], F32, name="bias")
         raw = [[keep.tile([P, PACK, RANK_T], F32, name="raw%d_%d" % (a, m)) for m in range(R)] for a in range(PASSES)]
         grouped = [keep.tile([P, T, PACK], BF16, name="grouped%d" % a, align_bytes=64) for a in range(PASSES)]
-        codes = [keep.tile([P, T], U32, name="codes%d" % a, align_bytes=64)[:] for a in range(SPLIT_PASSES)]
+        codes = [keep.tile([P, T], U32, name="codes%d" % a, align_bytes=64)[:] for a in range(LAST - 1)]
         late_codes = keep.tile([P, 2 * T], U32, name="late_codes", align_bytes=64)
         codes = codes + [late_codes[:, 0:T], late_codes[:, T:2 * T]]
         scales = keep.tile([P, T], U8, name="scales", align_bytes=64)
@@ -52,32 +54,31 @@ def tile_moe_eps_lin_silu_kernel(tc, xT, w_words, w_scales, b, offs, out):
         moved_scales = keep.tile([P, PASSES - 1, S], U8, name="moved_scales", align_bytes=64)
         w_codes = keep.tile([P, E * PASSES, 2 * N], U8, name="w_codes", align_bytes=64)
         w_planes = keep.tile([P, E * PASSES, N], U8, name="w_planes", align_bytes=64)
-        w_rows = keep.tile([16, E * PASSES, N // 4], I32, name="w_rows")
+        w_rows = keep.tile([4 * SCALE_ROWS, E * PASSES, N // 4], I32, name="w_rows")
         result = keep.tile([P, R, E * U], F32, name="result")
-        warm_in = keep.tile([P, 1], F32, name="warm_in")
-        warm_out = keep.tile([P, 1], F32, name="warm_out")
         banks = [psum.tile([P, U], F32, name="bank%d" % i) for i in range(BANKS)]
 
-        nc.vector.memset(warm_in[:], 0.0)
-        nc.scalar.activation(out=warm_out[:], in_=warm_in[:], func=ACT.Silu)
         nc.vector.memset(scales[:].bitcast(I32), 0)
         nc.vector.memset(w_planes[:].bitcast(I32), 0)
         nc.vector.memset(moved_scales[:].bitcast(I32), 0)
 
-        nc.scalar.dma_start(out=bias[:], in_=b)
         for a in range(PASSES):
             rows = xT[a * K_PASS:(a + 1) * K_PASS, :].rearrange("(p j) t -> p j t", j=PACK)
             for m in range(R):
                 nc.sync.dma_start(out=raw[a][m][:], in_=rows[:, :, m * RANK_T:(m + 1) * RANK_T])
                 if a == 0 and m == 0:
                     nc.sync.dma_start(offsets[:], offs)
+        nc.sync.dma_start(out=bias[:], in_=b)
         nc.sync.dma_start(out=w_rows[:], in_=w_scales.rearrange("e a q n -> q (e a) n").bitcast(I32))
         word_rows = w_words.rearrange("e a p c -> p (e a) c").bitcast(I32)
         for pair in range(E // 2):
             mats = slice(2 * pair * PASSES, 2 * (pair + 1) * PASSES)
             nc.sync.dma_start(out=w_codes[:, mats, :].bitcast(I32), in_=word_rows[:, mats, :])
-        for quad in range(4):
-            nc.sync.dma_start(out=w_planes[32 * quad:32 * quad + 4].bitcast(I32), in_=w_rows[4 * quad:4 * quad + 4])
+        for quad in range(P // QUADRANT):
+            nc.sync.dma_start(
+                out=w_planes[QUADRANT * quad:QUADRANT * quad + SCALE_ROWS].bitcast(I32),
+                in_=w_rows[SCALE_ROWS * quad:SCALE_ROWS * (quad + 1)],
+            )
 
         def cast(a, m, lo, hi, on_vector):
             dst = grouped[a][:, m * RANK_T + lo:m * RANK_T + hi, :].rearrange("p (c i) j -> p c j i", i=4)
@@ -91,31 +92,30 @@ def tile_moe_eps_lin_silu_kernel(tc, xT, w_words, w_scales, b, offs, out):
             cols = slice(m * RANK_T + lo, m * RANK_T + hi)
             nc.vector.quantize_mx(
                 out=codes[a][:, cols].bitcast(FP8X4),
-                scales=scales[4 * a:P, cols],
+                scales=scales[SCALE_ROWS * a:P, cols],
                 in_=grouped[a][:, cols, :].rearrange("p t j -> p (t j)"),
             )
 
         def gather(dst, window, lo, hi):
-            nc.vector.tensor_copy(dst[:, lo:hi], window.indirect(offsets[:, lo // 16:hi // 16]))
+            nc.vector.tensor_copy(dst[:, lo:hi], window.indirect(offsets[:, lo // LIST_GROUP:hi // LIST_GROUP]))
 
+        held_back = S - PAIR + U
         for a in range(PASSES):
             for m in range(R):
-                on_scalar, on_vector, quantised = SHARED if a == 0 else TAIL_SHARED if a >= SPLIT_PASSES and m == R - 1 else SCALAR_ONLY
+                last_load = a == LAST and m == R - 1
+                on_scalar, on_vector, quantised = FIRST_PASS if a == 0 else LAST_LOAD if last_load else SCALAR_ALONE
                 for lo, hi in on_scalar:
                     cast(a, m, lo, hi, False)
                 for lo, hi in on_vector:
                     cast(a, m, lo, hi, True)
                 for lo, hi in quantised:
                     quantize(a, m, lo, hi)
-                if a < SPLIT_PASSES:
+                if a < LAST:
                     for first in range(0, S, PAIR):
                         if m == 0:
                             gather(slot_codes[a], codes[a][:, 0:RANK_T], first, first + U)
-                        else:
+                        elif a < LAST - 1 or first + U < held_back:
                             gather(slot_codes[a], codes[a], first + U, first + PAIR)
-            if SPLIT_PASSES <= a < LAST:
-                for lo, hi in WORD_PIECES:
-                    gather(slot_codes[a], codes[a], lo, hi)
 
         def multiply(e, m, a):
             cols = slice(e * C + m * U, e * C + (m + 1) * U)
@@ -132,19 +132,19 @@ def tile_moe_eps_lin_silu_kernel(tc, xT, w_words, w_scales, b, offs, out):
 
         out_by_rank = out.rearrange("n (m x) -> n m x", m=R)
 
-        def scale_piece(e_lo, e_hi):
+        def gather_scales(e_lo, e_hi):
             lo, hi = e_lo * C, e_hi * C
             for first in range(lo, hi, PAIR):
                 gather(slot_scales, scales[:], first, first + PAIR)
             for a in range(1, PASSES):
                 nc.sync.dma_start(
-                    out=moved_scales[0:SHIFT_ROWS, a - 1, lo:hi].bitcast(I32),
-                    in_=slot_scales[4 * a:4 * a + SHIFT_ROWS, lo:hi].bitcast(I32),
+                    out=moved_scales[0:MOVED_ROWS, a - 1, lo:hi].bitcast(I32),
+                    in_=slot_scales[SCALE_ROWS * a:SCALE_ROWS * a + MOVED_ROWS, lo:hi].bitcast(I32),
                 )
 
-        def early(experts, passes):
+        def accumulate(e_lo, e_hi, passes):
             for a in passes:
-                for e in experts:
+                for e in range(e_lo, e_hi):
                     for m in range(R):
                         multiply(e, m, a)
 
@@ -165,15 +165,16 @@ def tile_moe_eps_lin_silu_kernel(tc, xT, w_words, w_scales, b, offs, out):
             if e_hi < E:
                 nc.sync.dma_start(out=out_by_rank[:, :, cols], in_=result[:, :, cols])
 
-        scale_piece(0, 4)
-        early(range(0, 4), (0,))
-        scale_piece(4, 8)
-        early(range(0, 4), (1, 2))
+        half = E // 2
+        gather_scales(0, half)
+        accumulate(0, half, range(0, 1))
+        gather_scales(half, E)
+        accumulate(0, half, range(1, LAST))
         finish(0, 2)
-        finish(2, 4)
-        early(range(4, 6), (0, 1, 2))
-        finish(4, 6)
-        gather(slot_codes[LAST - 1], late_codes[:], 6 * C, S)
-        early(range(6, 8), (0, 1, 2))
-        finish(6, 7)
-        finish(7, 8)
+        finish(2, half)
+        accumulate(half, E - 2, range(LAST))
+        finish(half, E - 2)
+        gather(slot_codes[LAST - 1], late_codes[:], held_back, S)
+        accumulate(E - 2, E, range(LAST))
+        finish(E - 2, E - 1)
+        finish(E - 1, E)

@@ -24,15 +24,19 @@ LAST = PASSES - 1
 RANK_T = T // R
 U = C // R
 PAIR = 2 * C
+PAIRS = E // 2
+LATE = PAIR - U
 LIST_GROUP = 16
 QUADRANT = 32
 SCALE_ROWS = 4
-MOVED_ROWS = 112
-BANKS = 8
+LAST_GATHER = T // 8
 
-FIRST_PASS = ([(0, 256)], [(256, 640)], [(256, 512), (512, 640), (0, 256)])
+FIRST_PASS = ([(0, 256)], [(256, 512), (512, 640)], [(256, 512), (0, 256), (512, 640)])
 SCALAR_ALONE = ([(0, 512), (512, 640)], [], [(0, 512), (512, 640)])
-LAST_LOAD = ([(0, 256), (256, 384)], [(384, 640)], [(384, 640), (0, 256), (256, 384)])
+
+WHOLE = [(0, 112)]
+SHORT = [(0, 4), (32, 36), (36, 100)]
+MOVES = [[WHOLE, WHOLE, WHOLE], [SHORT, WHOLE, WHOLE], [WHOLE, SHORT, SHORT]]
 
 
 def tile_moe_eps_lin_silu_kernel(tc, xT, w_words, w_scales, b, offs, out):
@@ -43,24 +47,28 @@ def tile_moe_eps_lin_silu_kernel(tc, xT, w_words, w_scales, b, offs, out):
 
         offsets = keep.tile([P, S // LIST_GROUP], U16, name="offsets")
         bias = keep.tile([P, E], F32, name="bias")
-        raw = [[keep.tile([P, PACK, RANK_T], F32, name="raw%d_%d" % (a, m)) for m in range(R)] for a in range(PASSES)]
+        raw = [
+            [keep.tile([P, PACK, RANK_T], F32, name="raw%d_%d" % (a, m), align_bytes=64) for m in range(R)]
+            for a in range(PASSES)
+        ]
         grouped = [keep.tile([P, T, PACK], BF16, name="grouped%d" % a, align_bytes=64) for a in range(PASSES)]
         codes = [keep.tile([P, T], U32, name="codes%d" % a, align_bytes=64)[:] for a in range(LAST - 1)]
-        late_codes = keep.tile([P, 2 * T], U32, name="late_codes", align_bytes=64)
-        codes = codes + [late_codes[:, 0:T], late_codes[:, T:2 * T]]
+        last_codes = keep.tile([P, 2 * T], U32, name="last_codes", align_bytes=64)
+        codes = codes + [last_codes[:, 0:T], last_codes[:, T:2 * T]]
         scales = keep.tile([P, T], U8, name="scales", align_bytes=64)
-        slot_codes = [keep.tile([P, S], U32, name="slot_codes%d" % a, align_bytes=64) for a in range(PASSES)]
-        slot_scales = keep.tile([P, S], U8, name="slot_scales", align_bytes=64)
-        moved_scales = keep.tile([P, PASSES - 1, S], U8, name="moved_scales", align_bytes=64)
-        w_codes = keep.tile([P, E * PASSES, 2 * N], U8, name="w_codes", align_bytes=64)
+        widths = [PAIRS * U, 2 * LATE, 2 * LATE]
+        slot_scales = [keep.tile([P, w], U8, name="slot_scales%d" % i, align_bytes=64) for i, w in enumerate(widths)]
+        moved = [keep.tile([P, LAST, w], U8, name="moved%d" % i, align_bytes=64) for i, w in enumerate(widths)]
+        w_codes = [keep.tile([P, E * PASSES // 2, 2 * N], U8, name="w_codes0", align_bytes=64)]
         w_planes = keep.tile([P, E * PASSES, N], U8, name="w_planes", align_bytes=64)
         w_rows = keep.tile([4 * SCALE_ROWS, E * PASSES, N // 4], I32, name="w_rows")
         result = keep.tile([P, R, E * U], F32, name="result")
-        banks = [psum.tile([P, U], F32, name="bank%d" % i) for i in range(BANKS)]
+        banks = [psum.tile([P, C], F32, name="bank%d" % e) for e in range(E)]
 
         nc.vector.memset(scales[:].bitcast(I32), 0)
         nc.vector.memset(w_planes[:].bitcast(I32), 0)
-        nc.vector.memset(moved_scales[:].bitcast(I32), 0)
+        for planes in moved:
+            nc.vector.memset(planes[:].bitcast(I32), 0)
 
         for a in range(PASSES):
             rows = xT[a * K_PASS:(a + 1) * K_PASS, :].rearrange("(p j) t -> p j t", j=PACK)
@@ -71,9 +79,16 @@ def tile_moe_eps_lin_silu_kernel(tc, xT, w_words, w_scales, b, offs, out):
         nc.sync.dma_start(out=bias[:], in_=b)
         nc.sync.dma_start(out=w_rows[:], in_=w_scales.rearrange("e a q n -> q (e a) n").bitcast(I32))
         word_rows = w_words.rearrange("e a p c -> p (e a) c").bitcast(I32)
-        for pair in range(E // 2):
-            mats = slice(2 * pair * PASSES, 2 * (pair + 1) * PASSES)
-            nc.sync.dma_start(out=w_codes[:, mats, :].bitcast(I32), in_=word_rows[:, mats, :])
+
+        def load_words(pair):
+            at = (pair % 2) * 2 * PASSES
+            nc.sync.dma_start(
+                out=w_codes[pair // 2][:, at:at + 2 * PASSES, :].bitcast(I32),
+                in_=word_rows[:, 2 * pair * PASSES:2 * (pair + 1) * PASSES, :],
+            )
+
+        load_words(0)
+        load_words(1)
         for quad in range(P // QUADRANT):
             nc.sync.dma_start(
                 out=w_planes[QUADRANT * quad:QUADRANT * quad + SCALE_ROWS].bitcast(I32),
@@ -97,84 +112,144 @@ def tile_moe_eps_lin_silu_kernel(tc, xT, w_words, w_scales, b, offs, out):
             )
 
         def gather(dst, window, lo, hi):
-            nc.vector.tensor_copy(dst[:, lo:hi], window.indirect(offsets[:, lo // LIST_GROUP:hi // LIST_GROUP]))
+            nc.vector.tensor_copy(dst, window.indirect(offsets[:, lo // LIST_GROUP:hi // LIST_GROUP]))
 
-        held_back = S - PAIR + U
+        slot_words = {}
+
+        def words_tile(a, lo, hi, tag=""):
+            piece = keep.tile([P, hi - lo], U32, name="words%d_%d" % (a, lo), tag=tag, align_bytes=64)
+            for first in range(lo, hi, U):
+                slot_words[a, first] = piece[:, first - lo:first - lo + U]
+            return piece
+
+        def gather_words(a, window, lo, hi, tag=""):
+            gather(words_tile(a, lo, hi, tag)[:], window, lo, hi)
+
+        def move_planes(i):
+            for a in range(1, PASSES):
+                for lo, hi in MOVES[i][a - 1]:
+                    nc.sync.dma_start(
+                        out=moved[i][lo:hi, a - 1, :].bitcast(I32),
+                        in_=slot_scales[i][SCALE_ROWS * a + lo:SCALE_ROWS * a + hi, :].bitcast(I32),
+                    )
+
+        def plane(e, m, a):
+            pair, at = divmod(e * C + m * U, PAIR)
+            i, col = (0, pair * U) if at == 0 else (1 + pair // 2, (pair % 2) * LATE + at - U)
+            return slot_scales[i][:, col:col + U] if a == 0 else moved[i][:, a - 1, col:col + U]
+
+        def multiply(e, m, a):
+            nc.tensor.matmul_mx(
+                out=banks[e][:, m * U:(m + 1) * U],
+                lhsT=w_codes[e // (E // 2)][:, (e % (E // 2)) * PASSES + a, :].bitcast(FP4X4),
+                lhsT_scale=w_planes[:, e * PASSES + a, :],
+                rhs=slot_words[a, e * C + m * U].bitcast(FP8X4),
+                rhs_scale=plane(e, m, a),
+                start=(a == 0 and m == (e + 1) % 2),
+                stop=(a == LAST and m == R - 1),
+            )
+
+        waiting = []
         for a in range(PASSES):
             for m in range(R):
-                last_load = a == LAST and m == R - 1
-                on_scalar, on_vector, quantised = FIRST_PASS if a == 0 else LAST_LOAD if last_load else SCALAR_ALONE
+                on_scalar, on_vector, quantised = FIRST_PASS if a == 0 else SCALAR_ALONE
                 for lo, hi in on_scalar:
                     cast(a, m, lo, hi, False)
                 for lo, hi in on_vector:
                     cast(a, m, lo, hi, True)
                 for lo, hi in quantised:
                     quantize(a, m, lo, hi)
-                if a < LAST:
-                    for first in range(0, S, PAIR):
-                        if m == 0:
-                            gather(slot_codes[a], codes[a][:, 0:RANK_T], first, first + U)
-                        elif a < LAST - 1 or first + U < held_back:
-                            gather(slot_codes[a], codes[a], first + U, first + PAIR)
+                if waiting:
+                    gather_words(*waiting.pop(), tag="raw%d_%d" % (a, m))
+                pieces = []
+                if m == 0:
+                    pieces = [(a, codes[a][:, 0:RANK_T], first, first + U) for first in range(0, S, PAIR)]
+                elif a < LAST:
+                    pairs = PAIRS - 1 if a == LAST - 1 else PAIRS
+                    pieces = [(a, codes[a], pair * PAIR + U, (pair + 1) * PAIR) for pair in range(pairs)]
+                if a == LAST and m == 0:
+                    for pair in range(PAIRS):
+                        early = slot_scales[0][:, pair * U:(pair + 1) * U]
+                        gather(early, scales[:, 0:RANK_T], pair * PAIR, pair * PAIR + U)
+                    move_planes(0)
+                if m == 0 or a < LAST - 1:
+                    waiting.append(pieces.pop())
+                for piece in pieces:
+                    gather_words(*piece)
 
-        def multiply(e, m, a):
-            cols = slice(e * C + m * U, e * C + (m + 1) * U)
-            plane = slot_scales[:, cols] if a == 0 else moved_scales[:, a - 1, cols]
-            nc.tensor.matmul_mx(
-                out=banks[(R * e + m) % BANKS][:],
-                lhsT=w_codes[:, e * PASSES + a, :].bitcast(FP4X4),
-                lhsT_scale=w_planes[:, e * PASSES + a, :],
-                rhs=slot_codes[a][:, cols].bitcast(FP8X4),
-                rhs_scale=plane,
-                start=(a == 0),
-                stop=(a == LAST),
-            )
-
+        w_codes.append(
+            keep.tile([P, E * PASSES // 2, 2 * N], U8, name="w_codes1", tag="grouped%d" % LAST, align_bytes=64)
+        )
+        load_words(2)
+        load_words(3)
         out_by_rank = out.rearrange("n (m x) -> n m x", m=R)
 
-        def gather_scales(e_lo, e_hi):
-            lo, hi = e_lo * C, e_hi * C
-            for first in range(lo, hi, PAIR):
-                gather(slot_scales, scales[:], first, first + PAIR)
-            for a in range(1, PASSES):
-                nc.sync.dma_start(
-                    out=moved_scales[0:MOVED_ROWS, a - 1, lo:hi].bitcast(I32),
-                    in_=slot_scales[SCALE_ROWS * a:SCALE_ROWS * a + MOVED_ROWS, lo:hi].bitcast(I32),
-                )
+        def gather_late_scales(half):
+            for pair in range(2 * half, 2 * half + 2):
+                at = (pair % 2) * LATE
+                gather(slot_scales[1 + half][:, at:at + LATE], scales[:], pair * PAIR + U, (pair + 1) * PAIR)
+            move_planes(1 + half)
 
-        def accumulate(e_lo, e_hi, passes):
+        def multiply_late(pairs, passes):
             for a in passes:
-                for e in range(e_lo, e_hi):
-                    for m in range(R):
-                        multiply(e, m, a)
+                for pair in pairs:
+                    multiply(2 * pair, 1, a)
+                    multiply(2 * pair + 1, 0, a)
+                    multiply(2 * pair + 1, 1, a)
 
-        def finish(e_lo, e_hi):
-            gather(slot_codes[LAST], codes[LAST], e_lo * C, e_hi * C)
-            for e in range(e_lo, e_hi):
-                for m in range(R):
-                    multiply(e, m, LAST)
-                    nc.scalar.activation(
-                        out=result[:, m, e * U:(e + 1) * U],
-                        in_=banks[(R * e + m) % BANKS][:],
-                        func=ACT.Silu,
-                        bias=bias[:, e:e + 1],
-                    )
-                    if e == E - 1:
-                        nc.sync.dma_start(out=out_by_rank[:, m, e * U:], in_=result[:, m, e * U:])
+        def open_pairs(pairs):
+            for pair in pairs:
+                multiply_late([pair], [0])
+                multiply(2 * pair, 0, 0)
+            for a in range(1, PASSES):
+                for pair in pairs:
+                    multiply(2 * pair, 0, a)
+
+        def activate(e):
+            nc.scalar.activation(
+                out=result[:, :, e * U:(e + 1) * U],
+                in_=banks[e][:].rearrange("p (m u) -> p m u", m=R),
+                func=ACT.Silu,
+                bias=bias[:, e:e + 1],
+            )
+
+        def store(e_lo, e_hi):
             cols = slice(e_lo * U, e_hi * U)
-            if e_hi < E:
-                nc.sync.dma_start(out=out_by_rank[:, :, cols], in_=result[:, :, cols])
+            nc.sync.dma_start(out=out_by_rank[:, :, cols], in_=result[:, :, cols])
 
-        half = E // 2
-        gather_scales(0, half)
-        accumulate(0, half, range(0, 1))
-        gather_scales(half, E)
-        accumulate(0, half, range(1, LAST))
-        finish(0, 2)
-        finish(2, half)
-        accumulate(half, E - 2, range(LAST))
-        finish(half, E - 2)
-        gather(slot_codes[LAST - 1], late_codes[:], held_back, S)
-        accumulate(E - 2, E, range(LAST))
-        finish(E - 2, E - 1)
-        finish(E - 1, E)
+        def close_pair(pair):
+            gather_words(LAST, codes[LAST], pair * PAIR + U, (pair + 1) * PAIR)
+            multiply(2 * pair, 1, LAST)
+            activate(2 * pair)
+            multiply(2 * pair + 1, 0, LAST)
+            multiply(2 * pair + 1, 1, LAST)
+            activate(2 * pair + 1)
+            store(2 * pair, 2 * pair + 2)
+
+        gather_late_scales(0)
+        open_pairs([0, 1])
+        gather_late_scales(1)
+        open_pairs([2, 3])
+        multiply_late([0, 1], [1, 2])
+        close_pair(0)
+        close_pair(1)
+        multiply_late([2, 3], [1])
+        gather_words(LAST - 1, last_codes[:], S - LATE, S)
+        multiply_late([2, 3], [2])
+        close_pair(2)
+
+        cut = S - LAST_GATHER
+        words = words_tile(LAST, S - LATE, S)
+        gather(words[:, 0:LATE - LAST_GATHER], codes[LAST], S - LATE, cut)
+        multiply(E - 2, 1, LAST)
+        activate(E - 2)
+        store(E - 2, E - 1)
+        gather(words[:, LATE - LAST_GATHER:], codes[LAST], cut, S)
+        e = E - 1
+        for m in range(R):
+            multiply(e, m, LAST)
+        for m in range(R):
+            nc.scalar.activation(
+                out=result[:, m, e * U:], in_=banks[e][:, m * U:(m + 1) * U], func=ACT.Silu, bias=bias[:, e:e + 1]
+            )
+            nc.sync.dma_start(out=out_by_rank[:, m, e * U:], in_=result[:, m, e * U:])

@@ -59,9 +59,7 @@ def tile_moe_eps_lin_silu_kernel(tc, xT, w_words, w_scales, b, offs, out):
         widths = [PAIRS * U, 2 * LATE, 2 * LATE]
         slot_scales = [keep.tile([P, w], U8, name="slot_scales%d" % i, align_bytes=64) for i, w in enumerate(widths)]
         moved = [keep.tile([P, LAST, w], U8, name="moved%d" % i, align_bytes=64) for i, w in enumerate(widths)]
-        w_codes = [keep.tile([P, E * PASSES // 2, 2 * N], U8, name="w_codes0", align_bytes=64)]
         w_planes = keep.tile([P, E * PASSES, N], U8, name="w_planes", align_bytes=64)
-        w_rows = keep.tile([4 * SCALE_ROWS, E * PASSES, N // 4], I32, name="w_rows")
         result = keep.tile([P, R, E * U], F32, name="result")
         banks = [psum.tile([P, C], F32, name="bank%d" % e) for e in range(E)]
 
@@ -77,23 +75,20 @@ def tile_moe_eps_lin_silu_kernel(tc, xT, w_words, w_scales, b, offs, out):
                 if a == 0 and m == 0:
                     nc.sync.dma_start(offsets[:], offs)
         nc.sync.dma_start(out=bias[:], in_=b)
-        nc.sync.dma_start(out=w_rows[:], in_=w_scales.rearrange("e a q n -> q (e a) n").bitcast(I32))
-        word_rows = w_words.rearrange("e a p c -> p (e a) c").bitcast(I32)
-
-        def load_words(pair):
-            at = (pair % 2) * 2 * PASSES
-            nc.sync.dma_start(
-                out=w_codes[pair // 2][:, at:at + 2 * PASSES, :].bitcast(I32),
-                in_=word_rows[:, 2 * pair * PASSES:2 * (pair + 1) * PASSES, :],
-            )
-
-        load_words(0)
-        load_words(1)
+        scale_rows = w_scales.rearrange("e a q n -> q (e a) n").bitcast(I32)
         for quad in range(P // QUADRANT):
             nc.sync.dma_start(
                 out=w_planes[QUADRANT * quad:QUADRANT * quad + SCALE_ROWS].bitcast(I32),
-                in_=w_rows[SCALE_ROWS * quad:SCALE_ROWS * (quad + 1)],
+                in_=scale_rows[SCALE_ROWS * quad:SCALE_ROWS * (quad + 1)],
             )
+
+        def load_words():
+            matrix_words = keep.tile([P, E * PASSES, 2 * N], U8, name="w_codes", tag="grouped1", align_bytes=64)
+            word_rows = w_words.rearrange("e a p c -> p (e a) c").bitcast(I32)
+            for pair in range(PAIRS):
+                matrices = slice(2 * pair * PASSES, 2 * (pair + 1) * PASSES)
+                nc.sync.dma_start(out=matrix_words[:, matrices, :].bitcast(I32), in_=word_rows[:, matrices, :])
+            return matrix_words
 
         def cast(a, m, lo, hi, on_vector):
             dst = grouped[a][:, m * RANK_T + lo:m * RANK_T + hi, :].rearrange("p (c i) j -> p c j i", i=4)
@@ -141,7 +136,7 @@ def tile_moe_eps_lin_silu_kernel(tc, xT, w_words, w_scales, b, offs, out):
         def multiply(e, m, a):
             nc.tensor.matmul_mx(
                 out=banks[e][:, m * U:(m + 1) * U],
-                lhsT=w_codes[e // (E // 2)][:, (e % (E // 2)) * PASSES + a, :].bitcast(FP4X4),
+                lhsT=w_codes[:, e * PASSES + a, :].bitcast(FP4X4),
                 lhsT_scale=w_planes[:, e * PASSES + a, :],
                 rhs=slot_words[a, e * C + m * U].bitcast(FP8X4),
                 rhs_scale=plane(e, m, a),
@@ -172,16 +167,13 @@ def tile_moe_eps_lin_silu_kernel(tc, xT, w_words, w_scales, b, offs, out):
                         early = slot_scales[0][:, pair * U:(pair + 1) * U]
                         gather(early, scales[:, 0:RANK_T], pair * PAIR, pair * PAIR + U)
                     move_planes(0)
+                if a == 1 and m == R - 1:
+                    w_codes = load_words()
                 if m == 0 or a < LAST - 1:
                     waiting.append(pieces.pop())
                 for piece in pieces:
                     gather_words(*piece)
 
-        w_codes.append(
-            keep.tile([P, E * PASSES // 2, 2 * N], U8, name="w_codes1", tag="grouped%d" % LAST, align_bytes=64)
-        )
-        load_words(2)
-        load_words(3)
         out_by_rank = out.rearrange("n (m x) -> n m x", m=R)
 
         def gather_late_scales(half):

@@ -26,6 +26,7 @@ U = C // R
 PAIR = 2 * C
 PAIRS = E // 2
 LATE = PAIR - U
+HALF = S // 2
 LIST_GROUP = 16
 QUADRANT = 32
 SCALE_ROWS = 4
@@ -33,6 +34,20 @@ LAST_GATHER = T // 8
 
 FIRST_PASS = ([(0, 256)], [(256, 512), (512, 640)], [(256, 512), (0, 256), (512, 640)])
 SCALAR_ALONE = ([(0, 512), (512, 640)], [], [(0, 512), (512, 640)])
+
+WINDOWS = [T, T, 2048, T]
+PIECES = [
+    [[(0, 128), (512, 640)], [(1152, 2048), (128, 512)]],
+    [[(0, 128), (512, 640), (1024, 1152)], [(128, 512), (640, 1024), (1152, 1536)]],
+    [[], [(128, 1536)]],
+    [[(0, 128)], []],
+]
+WAITING = [
+    [None, (0, 1024, 1152)],
+    [(0, 640, 1024), (1, 1536, 1664)],
+    [(1, 1664, 2048), (2, 0, 128)],
+    [(2, 1536, 1664), (3, 1024, 1152)],
+]
 
 WHOLE = [(0, 112)]
 SHORT = [(0, 4), (32, 36), (36, 100)]
@@ -52,11 +67,9 @@ def tile_moe_eps_lin_silu_kernel(tc, xT, w_words, w_scales, b, offs, out):
             for a in range(PASSES)
         ]
         grouped = [keep.tile([P, T, PACK], BF16, name="grouped%d" % a, align_bytes=64) for a in range(PASSES)]
-        codes = [keep.tile([P, T], U32, name="codes%d" % a, align_bytes=64)[:] for a in range(LAST - 1)]
-        last_codes = keep.tile([P, 2 * T], U32, name="last_codes", align_bytes=64)
-        codes = codes + [last_codes[:, 0:T], last_codes[:, T:2 * T]]
+        codes = [keep.tile([P, w], U32, name="codes%d" % a, align_bytes=64) for a, w in enumerate(WINDOWS)]
         scales = keep.tile([P, T], U8, name="scales", align_bytes=64)
-        widths = [PAIRS * U, 2 * LATE, 2 * LATE]
+        widths = [2 * U, HALF - U, HALF - U]
         slot_scales = [keep.tile([P, w], U8, name="slot_scales%d" % i, align_bytes=64) for i, w in enumerate(widths)]
         moved = [keep.tile([P, LAST, w], U8, name="moved%d" % i, align_bytes=64) for i, w in enumerate(widths)]
         w_planes = keep.tile([P, E * PASSES, N], U8, name="w_planes", align_bytes=64)
@@ -65,6 +78,7 @@ def tile_moe_eps_lin_silu_kernel(tc, xT, w_words, w_scales, b, offs, out):
 
         nc.vector.memset(scales[:].bitcast(I32), 0)
         nc.vector.memset(w_planes[:].bitcast(I32), 0)
+        nc.vector.memset(codes[LAST - 1][:, T:].bitcast(I32), 0)
         for planes in moved:
             nc.vector.memset(planes[:].bitcast(I32), 0)
 
@@ -117,8 +131,9 @@ def tile_moe_eps_lin_silu_kernel(tc, xT, w_words, w_scales, b, offs, out):
                 slot_words[a, first] = piece[:, first - lo:first - lo + U]
             return piece
 
-        def gather_words(a, window, lo, hi, tag=""):
-            gather(words_tile(a, lo, hi, tag)[:], window, lo, hi)
+        def gather_words(a, lo, hi, tag=""):
+            early = hi - lo == U
+            gather(words_tile(a, lo, hi, tag)[:], codes[a][:, 0:RANK_T] if early else codes[a][:], lo, hi)
 
         def move_planes(i):
             for a in range(1, PASSES):
@@ -129,8 +144,8 @@ def tile_moe_eps_lin_silu_kernel(tc, xT, w_words, w_scales, b, offs, out):
                     )
 
         def plane(e, m, a):
-            pair, at = divmod(e * C + m * U, PAIR)
-            i, col = (0, pair * U) if at == 0 else (1 + pair // 2, (pair % 2) * LATE + at - U)
+            half, at = divmod(e * C + m * U, HALF)
+            i, col = (0, half * U) if at == 0 else (1 + half, at - U)
             return slot_scales[i][:, col:col + U] if a == 0 else moved[i][:, a - 1, col:col + U]
 
         def multiply(e, m, a):
@@ -140,11 +155,10 @@ def tile_moe_eps_lin_silu_kernel(tc, xT, w_words, w_scales, b, offs, out):
                 lhsT_scale=w_planes[:, e * PASSES + a, :],
                 rhs=slot_words[a, e * C + m * U].bitcast(FP8X4),
                 rhs_scale=plane(e, m, a),
-                start=(a == 0 and m == (e + 1) % 2),
+                start=(a == 0 and m == (1 if e % (E // 2) == 0 else 0)),
                 stop=(a == LAST and m == R - 1),
             )
 
-        waiting = []
         for a in range(PASSES):
             for m in range(R):
                 on_scalar, on_vector, quantised = FIRST_PASS if a == 0 else SCALAR_ALONE
@@ -154,48 +168,34 @@ def tile_moe_eps_lin_silu_kernel(tc, xT, w_words, w_scales, b, offs, out):
                     cast(a, m, lo, hi, True)
                 for lo, hi in quantised:
                     quantize(a, m, lo, hi)
-                if waiting:
-                    gather_words(*waiting.pop(), tag="raw%d_%d" % (a, m))
-                pieces = []
-                if m == 0:
-                    pieces = [(a, codes[a][:, 0:RANK_T], first, first + U) for first in range(0, S, PAIR)]
-                elif a < LAST:
-                    pairs = PAIRS - 1 if a == LAST - 1 else PAIRS
-                    pieces = [(a, codes[a], pair * PAIR + U, (pair + 1) * PAIR) for pair in range(pairs)]
+                if WAITING[a][m]:
+                    gather_words(*WAITING[a][m], tag="raw%d_%d" % (a, m))
                 if a == LAST and m == 0:
-                    for pair in range(PAIRS):
-                        early = slot_scales[0][:, pair * U:(pair + 1) * U]
-                        gather(early, scales[:, 0:RANK_T], pair * PAIR, pair * PAIR + U)
+                    for half in range(2):
+                        early = slot_scales[0][:, half * U:(half + 1) * U]
+                        gather(early, scales[:, 0:RANK_T], half * HALF, half * HALF + U)
                     move_planes(0)
                 if a == 1 and m == R - 1:
                     w_codes = load_words()
-                if m == 0 or a < LAST - 1:
-                    waiting.append(pieces.pop())
-                for piece in pieces:
-                    gather_words(*piece)
+                for lo, hi in PIECES[a][m]:
+                    gather_words(a, lo, hi)
 
         out_by_rank = out.rearrange("n (m x) -> n m x", m=R)
 
         def gather_late_scales(half):
-            for pair in range(2 * half, 2 * half + 2):
-                at = (pair % 2) * LATE
-                gather(slot_scales[1 + half][:, at:at + LATE], scales[:], pair * PAIR + U, (pair + 1) * PAIR)
+            gather(slot_scales[1 + half][:], scales[:], half * HALF + U, (half + 1) * HALF)
             move_planes(1 + half)
 
         def multiply_late(pairs, passes):
             for a in passes:
                 for pair in pairs:
-                    multiply(2 * pair, 1, a)
-                    multiply(2 * pair + 1, 0, a)
-                    multiply(2 * pair + 1, 1, a)
+                    for first in range(pair * PAIR + (U if pair % 2 == 0 else 0), (pair + 1) * PAIR, U):
+                        multiply(first // C, (first // U) % R, a)
 
-        def open_pairs(pairs):
-            for pair in pairs:
-                multiply_late([pair], [0])
-                multiply(2 * pair, 0, 0)
-            for a in range(1, PASSES):
-                for pair in pairs:
-                    multiply(2 * pair, 0, a)
+        def open_half(half):
+            multiply_late([2 * half, 2 * half + 1], [0])
+            for a in range(PASSES):
+                multiply(half * E // 2, 0, a)
 
         def activate(e):
             nc.scalar.activation(
@@ -210,7 +210,9 @@ def tile_moe_eps_lin_silu_kernel(tc, xT, w_words, w_scales, b, offs, out):
             nc.sync.dma_start(out=out_by_rank[:, :, cols], in_=result[:, :, cols])
 
         def close_pair(pair):
-            gather_words(LAST, codes[LAST], pair * PAIR + U, (pair + 1) * PAIR)
+            gather_words(LAST, pair * PAIR + (U if pair % 2 == 0 else 0), (pair + 1) * PAIR)
+            if pair % 2 == 1:
+                multiply(2 * pair, 0, LAST)
             multiply(2 * pair, 1, LAST)
             activate(2 * pair)
             multiply(2 * pair + 1, 0, LAST)
@@ -219,24 +221,25 @@ def tile_moe_eps_lin_silu_kernel(tc, xT, w_words, w_scales, b, offs, out):
             store(2 * pair, 2 * pair + 2)
 
         gather_late_scales(0)
-        open_pairs([0, 1])
+        open_half(0)
         gather_late_scales(1)
-        open_pairs([2, 3])
+        open_half(1)
         multiply_late([0, 1], [1, 2])
         close_pair(0)
         close_pair(1)
         multiply_late([2, 3], [1])
-        gather_words(LAST - 1, last_codes[:], S - LATE, S)
+        gather_words(LAST - 1, S - LATE, S, tag="grouped%d" % LAST)
         multiply_late([2, 3], [2])
         close_pair(2)
 
         cut = S - LAST_GATHER
-        words = words_tile(LAST, S - LATE, S)
-        gather(words[:, 0:LATE - LAST_GATHER], codes[LAST], S - LATE, cut)
+        words = words_tile(LAST, S - PAIR, S)
+        gather(words[:, 0:PAIR - LAST_GATHER], codes[LAST][:], S - PAIR, cut)
+        multiply(E - 2, 0, LAST)
         multiply(E - 2, 1, LAST)
         activate(E - 2)
         store(E - 2, E - 1)
-        gather(words[:, LATE - LAST_GATHER:], codes[LAST], cut, S)
+        gather(words[:, PAIR - LAST_GATHER:], codes[LAST][:], cut, S)
         e = E - 1
         for m in range(R):
             multiply(e, m, LAST)

@@ -33,21 +33,24 @@ SCALE_ROWS = 4
 LAST_GATHER = T // 8
 
 FIRST_PASS = ([(0, 256)], [(256, 512), (512, 640)], [(256, 512), (0, 256), (512, 640)])
-SCALAR_ALONE = ([(0, 512), (512, 640)], [], [(0, 512), (512, 640)])
+SCALAR_ALONE = ([(0, 384), (512, 640)], [], [(0, 512), (512, 640)])
+ON_GPSIMD = (384, 512)
 
-WINDOWS = [T, T, 2048, T]
+WINDOWS = [T, T, T, T]
 PIECES = [
     [[(0, 128), (512, 640)], [(1152, 2048), (128, 512)]],
     [[(0, 128), (512, 640), (1024, 1152)], [(128, 512), (640, 1024), (1152, 1536)]],
-    [[], [(128, 1536)]],
-    [[(0, 128)], []],
+    [[(0, 128), (1024, 1152)], [(128, 1024), (1152, 1536)]],
+    [[(0, 128), (1024, 1152)], []],
 ]
 WAITING = [
     [None, (0, 1024, 1152)],
     [(0, 640, 1024), (1, 1536, 1664)],
-    [(1, 1664, 2048), (2, 0, 128)],
-    [(2, 1536, 1664), (3, 1024, 1152)],
+    [(1, 1664, 2048), (2, 1536, 1664)],
+    [None, (3, 1536, 1664)],
 ]
+EARLY = [0, 1024, 1536]
+LATE_SETS = [[(128, 1024)], [(1152, 1536), (1664, 2048)]]
 
 WHOLE = [(0, 112)]
 SHORT = [(0, 4), (32, 36), (36, 100)]
@@ -69,7 +72,7 @@ def tile_moe_eps_lin_silu_kernel(tc, xT, w_words, w_scales, b, offs, out):
         grouped = [keep.tile([P, T, PACK], BF16, name="grouped%d" % a, align_bytes=64) for a in range(PASSES)]
         codes = [keep.tile([P, w], U32, name="codes%d" % a, align_bytes=64) for a, w in enumerate(WINDOWS)]
         scales = keep.tile([P, T], U8, name="scales", align_bytes=64)
-        widths = [2 * U, HALF - U, HALF - U]
+        widths = [len(EARLY) * U, HALF - U, 2 * LATE]
         slot_scales = [keep.tile([P, w], U8, name="slot_scales%d" % i, align_bytes=64) for i, w in enumerate(widths)]
         moved = [keep.tile([P, LAST, w], U8, name="moved%d" % i, align_bytes=64) for i, w in enumerate(widths)]
         w_planes = keep.tile([P, E * PASSES, N], U8, name="w_planes", align_bytes=64)
@@ -78,7 +81,6 @@ def tile_moe_eps_lin_silu_kernel(tc, xT, w_words, w_scales, b, offs, out):
 
         nc.vector.memset(scales[:].bitcast(I32), 0)
         nc.vector.memset(w_planes[:].bitcast(I32), 0)
-        nc.vector.memset(codes[LAST - 1][:, T:].bitcast(I32), 0)
         for planes in moved:
             nc.vector.memset(planes[:].bitcast(I32), 0)
 
@@ -144,8 +146,12 @@ def tile_moe_eps_lin_silu_kernel(tc, xT, w_words, w_scales, b, offs, out):
                     )
 
         def plane(e, m, a):
-            half, at = divmod(e * C + m * U, HALF)
-            i, col = (0, half * U) if at == 0 else (1 + half, at - U)
+            first = e * C + m * U
+            if first in EARLY:
+                i, col = 0, EARLY.index(first) * U
+            else:
+                i = 1 + first // HALF
+                col = first % HALF - U * len([x for x in EARLY if first // HALF * HALF <= x < first])
             return slot_scales[i][:, col:col + U] if a == 0 else moved[i][:, a - 1, col:col + U]
 
         def multiply(e, m, a):
@@ -155,7 +161,7 @@ def tile_moe_eps_lin_silu_kernel(tc, xT, w_words, w_scales, b, offs, out):
                 lhsT_scale=w_planes[:, e * PASSES + a, :],
                 rhs=slot_words[a, e * C + m * U].bitcast(FP8X4),
                 rhs_scale=plane(e, m, a),
-                start=(a == 0 and m == (1 if e % (E // 2) == 0 else 0)),
+                start=(a == 0 and m == (1 if e * C in EARLY else 0)),
                 stop=(a == LAST and m == R - 1),
             )
 
@@ -166,14 +172,19 @@ def tile_moe_eps_lin_silu_kernel(tc, xT, w_words, w_scales, b, offs, out):
                     cast(a, m, lo, hi, False)
                 for lo, hi in on_vector:
                     cast(a, m, lo, hi, True)
+                if a > 0:
+                    lo, hi = ON_GPSIMD
+                    nc.gpsimd.tensor_copy(
+                        out=grouped[a][:, m * RANK_T + lo:m * RANK_T + hi, :],
+                        in_=raw[a][m][:, :, lo:hi].rearrange("p j t -> p t j"),
+                    )
                 for lo, hi in quantised:
                     quantize(a, m, lo, hi)
                 if WAITING[a][m]:
                     gather_words(*WAITING[a][m], tag="raw%d_%d" % (a, m))
                 if a == LAST and m == 0:
-                    for half in range(2):
-                        early = slot_scales[0][:, half * U:(half + 1) * U]
-                        gather(early, scales[:, 0:RANK_T], half * HALF, half * HALF + U)
+                    for i, first in enumerate(EARLY):
+                        gather(slot_scales[0][:, i * U:(i + 1) * U], scales[:, 0:RANK_T], first, first + U)
                     move_planes(0)
                 if a == 1 and m == R - 1:
                     w_codes = load_words()
@@ -183,19 +194,24 @@ def tile_moe_eps_lin_silu_kernel(tc, xT, w_words, w_scales, b, offs, out):
         out_by_rank = out.rearrange("n (m x) -> n m x", m=R)
 
         def gather_late_scales(half):
-            gather(slot_scales[1 + half][:], scales[:], half * HALF + U, (half + 1) * HALF)
+            at = 0
+            for lo, hi in LATE_SETS[half]:
+                gather(slot_scales[1 + half][:, at:at + hi - lo], scales[:], lo, hi)
+                at = at + hi - lo
             move_planes(1 + half)
 
         def multiply_late(pairs, passes):
             for a in passes:
                 for pair in pairs:
-                    for first in range(pair * PAIR + (U if pair % 2 == 0 else 0), (pair + 1) * PAIR, U):
+                    for first in range(pair * PAIR + (U if pair * PAIR in EARLY else 0), (pair + 1) * PAIR, U):
                         multiply(first // C, (first // U) % R, a)
 
         def open_half(half):
             multiply_late([2 * half, 2 * half + 1], [0])
             for a in range(PASSES):
-                multiply(half * E // 2, 0, a)
+                for first in EARLY:
+                    if first // HALF == half:
+                        multiply(first // C, 0, a)
 
         def activate(e):
             nc.scalar.activation(
@@ -210,8 +226,8 @@ def tile_moe_eps_lin_silu_kernel(tc, xT, w_words, w_scales, b, offs, out):
             nc.sync.dma_start(out=out_by_rank[:, :, cols], in_=result[:, :, cols])
 
         def close_pair(pair):
-            gather_words(LAST, pair * PAIR + (U if pair % 2 == 0 else 0), (pair + 1) * PAIR)
-            if pair % 2 == 1:
+            gather_words(LAST, pair * PAIR + (U if pair * PAIR in EARLY else 0), (pair + 1) * PAIR)
+            if pair * PAIR not in EARLY:
                 multiply(2 * pair, 0, LAST)
             multiply(2 * pair, 1, LAST)
             activate(2 * pair)
@@ -233,13 +249,12 @@ def tile_moe_eps_lin_silu_kernel(tc, xT, w_words, w_scales, b, offs, out):
         close_pair(2)
 
         cut = S - LAST_GATHER
-        words = words_tile(LAST, S - PAIR, S)
-        gather(words[:, 0:PAIR - LAST_GATHER], codes[LAST][:], S - PAIR, cut)
-        multiply(E - 2, 0, LAST)
+        words = words_tile(LAST, S - LATE, S)
+        gather(words[:, 0:LATE - LAST_GATHER], codes[LAST][:], S - LATE, cut)
         multiply(E - 2, 1, LAST)
         activate(E - 2)
         store(E - 2, E - 1)
-        gather(words[:, PAIR - LAST_GATHER:], codes[LAST][:], cut, S)
+        gather(words[:, LATE - LAST_GATHER:], codes[LAST][:], cut, S)
         e = E - 1
         for m in range(R):
             multiply(e, m, LAST)

@@ -33,14 +33,14 @@ SCALE_ROWS = 4
 LAST_GATHER = T // 8
 
 FIRST_PASS = ([(0, 256)], [(256, 512), (512, 640)], [(256, 512), (0, 256), (512, 640)])
-SCALAR_ALONE = ([(0, 384), (512, 640)], [], [(0, 512), (512, 640)])
-ON_GPSIMD = (384, 512)
+SCALAR_ALONE = ([(0, 352), (512, 640)], [], [(0, 512), (512, 640)])
+ON_GPSIMD = (352, 512)
 
 WINDOWS = [T, T, T, T]
 PIECES = [
     [[(0, 128), (512, 640)], [(1152, 2048), (128, 512)]],
+    [[(0, 128), (256, 384), (512, 640), (1024, 1152)], [(128, 256), (384, 512), (640, 1024), (1152, 1536)]],
     [[(0, 128), (512, 640), (1024, 1152)], [(128, 512), (640, 1024), (1152, 1536)]],
-    [[(0, 128), (1024, 1152)], [(128, 1024), (1152, 1536)]],
     [[(0, 128), (1024, 1152)], []],
 ]
 WAITING = [
@@ -49,8 +49,9 @@ WAITING = [
     [(1, 1664, 2048), (2, 1536, 1664)],
     [None, (3, 1536, 1664)],
 ]
-EARLY = [0, 1024, 1536]
-LATE_SETS = [[(128, 1024)], [(1152, 1536), (1664, 2048)]]
+EARLY = [1024, 1536]
+EARLY_WORDS = [0, 1024, 1536]
+LATE_SETS = [[(0, 1024)], [(1152, 1536), (1664, 2048)]]
 
 WHOLE = [(0, 112)]
 SHORT = [(0, 4), (32, 36), (36, 100)]
@@ -71,8 +72,8 @@ def tile_moe_eps_lin_silu_kernel(tc, xT, w_words, w_scales, b, offs, out):
         ]
         grouped = [keep.tile([P, T, PACK], BF16, name="grouped%d" % a, align_bytes=64) for a in range(PASSES)]
         codes = [keep.tile([P, w], U32, name="codes%d" % a, align_bytes=64) for a, w in enumerate(WINDOWS)]
-        scales = keep.tile([P, T], U8, name="scales", align_bytes=64)
-        widths = [len(EARLY) * U, HALF - U, 2 * LATE]
+        scales = keep.tile([P, T + U], U8, name="scales", align_bytes=64)
+        widths = [len(EARLY) * U, HALF, 2 * LATE]
         slot_scales = [keep.tile([P, w], U8, name="slot_scales%d" % i, align_bytes=64) for i, w in enumerate(widths)]
         moved = [keep.tile([P, LAST, w], U8, name="moved%d" % i, align_bytes=64) for i, w in enumerate(widths)]
         w_planes = keep.tile([P, E * PASSES, N], U8, name="w_planes", align_bytes=64)
@@ -134,7 +135,7 @@ def tile_moe_eps_lin_silu_kernel(tc, xT, w_words, w_scales, b, offs, out):
             return piece
 
         def gather_words(a, lo, hi, tag=""):
-            early = hi - lo == U
+            early = hi - lo == U and lo % C == 0
             gather(words_tile(a, lo, hi, tag)[:], codes[a][:, 0:RANK_T] if early else codes[a][:], lo, hi)
 
         def move_planes(i):
@@ -226,7 +227,7 @@ def tile_moe_eps_lin_silu_kernel(tc, xT, w_words, w_scales, b, offs, out):
             nc.sync.dma_start(out=out_by_rank[:, :, cols], in_=result[:, :, cols])
 
         def close_pair(pair):
-            gather_words(LAST, pair * PAIR + (U if pair * PAIR in EARLY else 0), (pair + 1) * PAIR)
+            gather_words(LAST, pair * PAIR + (U if pair * PAIR in EARLY_WORDS else 0), (pair + 1) * PAIR)
             if pair * PAIR not in EARLY:
                 multiply(2 * pair, 0, LAST)
             multiply(2 * pair, 1, LAST)

@@ -33,24 +33,23 @@ SCALE_ROWS = 4
 LAST_GATHER = T // 8
 
 FIRST_PASS = ([(0, 256)], [(256, 512), (512, 640)], [(256, 512), (0, 256), (512, 640)])
-SCALAR_ALONE = ([(0, 352), (512, 640)], [], [(0, 512), (512, 640)])
-ON_GPSIMD = (352, 512)
+SCALAR_ALONE = ([(0, 384), (512, 640)], [], [(0, 512), (512, 640)])
+ON_GPSIMD = (384, 512)
 
 WINDOWS = [T, T, T, T]
 PIECES = [
-    [[(0, 128), (512, 640)], [(1152, 2048), (128, 512)]],
     [[(0, 128), (256, 384), (512, 640), (1024, 1152)], [(128, 256), (384, 512), (640, 1024), (1152, 1536)]],
-    [[(0, 128), (512, 640), (1024, 1152)], [(128, 512), (640, 1024), (1152, 1536)]],
-    [[(0, 128), (1024, 1152)], []],
+    [[(0, 128), (256, 384), (512, 640), (1024, 1152)], [(128, 256), (384, 512), (640, 1024), (1152, 1536)]],
+    [[(0, 128), (1024, 1152)], [(128, 1024), (1152, 1536)]],
+    [[(1024, 1152)], []],
 ]
 WAITING = [
-    [None, (0, 1024, 1152)],
-    [(0, 640, 1024), (1, 1536, 1664)],
+    [None, (0, 1536, 1664)],
+    [(0, 1664, 2048), (1, 1536, 1664)],
     [(1, 1664, 2048), (2, 1536, 1664)],
     [None, (3, 1536, 1664)],
 ]
 EARLY = [1024, 1536]
-EARLY_WORDS = [0, 1024, 1536]
 LATE_SETS = [[(0, 1024)], [(1152, 1536), (1664, 2048)]]
 
 WHOLE = [(0, 112)]
@@ -227,7 +226,7 @@ def tile_moe_eps_lin_silu_kernel(tc, xT, w_words, w_scales, b, offs, out):
             nc.sync.dma_start(out=out_by_rank[:, :, cols], in_=result[:, :, cols])
 
         def close_pair(pair):
-            gather_words(LAST, pair * PAIR + (U if pair * PAIR in EARLY_WORDS else 0), (pair + 1) * PAIR)
+            gather_words(LAST, pair * PAIR + (U if pair * PAIR in EARLY else 0), (pair + 1) * PAIR)
             if pair * PAIR not in EARLY:
                 multiply(2 * pair, 0, LAST)
             multiply(2 * pair, 1, LAST)

@@ -33,20 +33,20 @@ SCALE_ROWS = 4
 LAST_GATHER = T // 8
 
 FIRST_PASS = ([(0, 256)], [(256, 512), (512, 640)], [(256, 512), (0, 256), (512, 640)])
-SCALAR_ALONE = ([(0, 384), (512, 640)], [], [(0, 512), (512, 640)])
-ON_GPSIMD = (384, 512)
+SCALAR_ALONE = ([(0, 320), (512, 640)], [], [(0, 512), (512, 640)])
+ON_GPSIMD = (320, 512)
 
 WINDOWS = [T, T, T, T]
 PIECES = [
     [[(0, 128), (256, 384), (512, 640), (1024, 1152)], [(128, 256), (384, 512), (640, 1024), (1152, 1536)]],
     [[(0, 128), (256, 384), (512, 640), (1024, 1152)], [(128, 256), (384, 512), (640, 1024), (1152, 1536)]],
-    [[(0, 128), (1024, 1152)], [(128, 1024), (1152, 1536)]],
+    [[(0, 128), (512, 640)], [(128, 512), (640, 1024), (1152, 1792)]],
     [[(1024, 1152)], []],
 ]
 WAITING = [
     [None, (0, 1536, 1664)],
     [(0, 1664, 2048), (1, 1536, 1664)],
-    [(1, 1664, 2048), (2, 1536, 1664)],
+    [(1, 1664, 2048), (2, 1024, 1152)],
     [None, (3, 1536, 1664)],
 ]
 EARLY = [1024, 1536]
@@ -244,7 +244,7 @@ def tile_moe_eps_lin_silu_kernel(tc, xT, w_words, w_scales, b, offs, out):
         close_pair(0)
         close_pair(1)
         multiply_late([2, 3], [1])
-        gather_words(LAST - 1, S - LATE, S, tag="grouped%d" % LAST)
+        gather_words(LAST - 1, S - C, S, tag="grouped%d" % LAST)
         multiply_late([2, 3], [2])
         close_pair(2)
 

@@ -33,24 +33,12 @@ SCALE_ROWS = 4
 LAST_GATHER = T // 8
 
 FIRST_PASS = ([(0, 256)], [(256, 512), (512, 640)], [(256, 512), (0, 256), (512, 640)])
-SCALAR_ALONE = ([(0, 320), (512, 640)], [], [(0, 512), (512, 640)])
+LATER_PASSES = ([(0, 320), (512, 640)], [], [(0, 512), (512, 640)])
 ON_GPSIMD = (320, 512)
 
-WINDOWS = [T, T, T, T]
-PIECES = [
-    [[(0, 128), (256, 384), (512, 640), (1024, 1152)], [(128, 256), (384, 512), (640, 1024), (1152, 1536)]],
-    [[(0, 128), (256, 384), (512, 640), (1024, 1152)], [(128, 256), (384, 512), (640, 1024), (1152, 1536)]],
-    [[(0, 128), (512, 640)], [(128, 512), (640, 1024), (1152, 1792)]],
-    [[(1024, 1152)], []],
-]
-WAITING = [
-    [None, (0, 1536, 1664)],
-    [(0, 1664, 2048), (1, 1536, 1664)],
-    [(1, 1664, 2048), (2, 1024, 1152)],
-    [None, (3, 1536, 1664)],
-]
-EARLY = [1024, 1536]
-LATE_SETS = [[(0, 1024)], [(1152, 1536), (1664, 2048)]]
+EARLY_EXPERTS = [[0, 1, 2, 4, 6], [0, 2, 4, 6], [0, 4], [4, 6]]
+EARLY = [e * C for e in EARLY_EXPERTS[LAST]]
+HELD = C
 
 WHOLE = [(0, 112)]
 SHORT = [(0, 4), (32, 36), (36, 100)]
@@ -70,7 +58,7 @@ def tile_moe_eps_lin_silu_kernel(tc, xT, w_words, w_scales, b, offs, out):
             for a in range(PASSES)
         ]
         grouped = [keep.tile([P, T, PACK], BF16, name="grouped%d" % a, align_bytes=64) for a in range(PASSES)]
-        codes = [keep.tile([P, w], U32, name="codes%d" % a, align_bytes=64) for a, w in enumerate(WINDOWS)]
+        codes = [keep.tile([P, T], U32, name="codes%d" % a, align_bytes=64) for a in range(PASSES)]
         scales = keep.tile([P, T + U], U8, name="scales", align_bytes=64)
         widths = [len(EARLY) * U, HALF, 2 * LATE]
         slot_scales = [keep.tile([P, w], U8, name="slot_scales%d" % i, align_bytes=64) for i, w in enumerate(widths)]
@@ -134,8 +122,12 @@ def tile_moe_eps_lin_silu_kernel(tc, xT, w_words, w_scales, b, offs, out):
             return piece
 
         def gather_words(a, lo, hi, tag=""):
-            early = hi - lo == U and lo % C == 0
-            gather(words_tile(a, lo, hi, tag)[:], codes[a][:, 0:RANK_T] if early else codes[a][:], lo, hi)
+            rank0_alone = hi - lo == U and lo % C == 0
+            gather(words_tile(a, lo, hi, tag)[:], codes[a][:, 0:RANK_T] if rank0_alone else codes[a][:], lo, hi)
+
+        def late_runs(a, lo, hi):
+            edges = [lo] + [x for e in EARLY_EXPERTS[a] if lo <= e * C < hi for x in (e * C, e * C + U)] + [hi]
+            return [(x, y) for x, y in zip(edges[0::2], edges[1::2]) if x < y]
 
         def move_planes(i):
             for a in range(1, PASSES):
@@ -165,9 +157,10 @@ def tile_moe_eps_lin_silu_kernel(tc, xT, w_words, w_scales, b, offs, out):
                 stop=(a == LAST and m == R - 1),
             )
 
+        waiting = []
         for a in range(PASSES):
             for m in range(R):
-                on_scalar, on_vector, quantised = FIRST_PASS if a == 0 else SCALAR_ALONE
+                on_scalar, on_vector, quantised = FIRST_PASS if a == 0 else LATER_PASSES
                 for lo, hi in on_scalar:
                     cast(a, m, lo, hi, False)
                 for lo, hi in on_vector:
@@ -180,22 +173,29 @@ def tile_moe_eps_lin_silu_kernel(tc, xT, w_words, w_scales, b, offs, out):
                     )
                 for lo, hi in quantised:
                     quantize(a, m, lo, hi)
-                if WAITING[a][m]:
-                    gather_words(*WAITING[a][m], tag="raw%d_%d" % (a, m))
+                if waiting:
+                    gather_words(*waiting.pop(), tag="raw%d_%d" % (a, m))
                 if a == LAST and m == 0:
                     for i, first in enumerate(EARLY):
                         gather(slot_scales[0][:, i * U:(i + 1) * U], scales[:, 0:RANK_T], first, first + U)
                     move_planes(0)
                 if a == 1 and m == R - 1:
                     w_codes = load_words()
-                for lo, hi in PIECES[a][m]:
+                runs = []
+                if m == 0:
+                    runs = [(e * C, e * C + U) for e in EARLY_EXPERTS[a]]
+                elif a < LAST:
+                    runs = late_runs(a, 0, S - HELD if a == LAST - 1 else S)
+                if m == 0 or a < LAST - 1:
+                    waiting.append((a, *runs.pop()))
+                for lo, hi in runs:
                     gather_words(a, lo, hi)
 
         out_by_rank = out.rearrange("n (m x) -> n m x", m=R)
 
         def gather_late_scales(half):
             at = 0
-            for lo, hi in LATE_SETS[half]:
+            for lo, hi in late_runs(LAST, half * HALF, (half + 1) * HALF):
                 gather(slot_scales[1 + half][:, at:at + hi - lo], scales[:], lo, hi)
                 at = at + hi - lo
             move_planes(1 + half)
@@ -244,7 +244,7 @@ def tile_moe_eps_lin_silu_kernel(tc, xT, w_words, w_scales, b, offs, out):
         close_pair(0)
         close_pair(1)
         multiply_late([2, 3], [1])
-        gather_words(LAST - 1, S - C, S, tag="grouped%d" % LAST)
+        gather_words(LAST - 1, S - HELD, S, tag="grouped%d" % LAST)
         multiply_late([2, 3], [2])
         close_pair(2)
 

@@ -32,17 +32,22 @@ QUADRANT = 32
 SCALE_ROWS = 4
 LAST_GATHER = T // 8
 
-FIRST_PASS = ([(0, 256)], [(256, 512), (512, 640)], [(256, 512), (0, 256), (512, 640)])
-LATER_PASSES = ([(0, 320), (512, 640)], [], [(0, 512), (512, 640)])
-ON_GPSIMD = (320, 512)
+FIRST_PASS = ([(0, 256)], [(256, 512), (512, 640)], [], [(256, 512), (0, 256), (512, 640)])
+LATER_PASSES = ([(0, 352), (512, 640)], [], [(352, 512)], [(0, 512), (512, 640)])
+LAST_CUT = 384
+LAST_LOAD = ([(0, 256), (256, 384), (384, 512), (512, 640)], [], [], [(0, 256), (256, 512), (512, 640)])
 
-EARLY_EXPERTS = [[0, 1, 2, 4, 6], [0, 2, 4, 6], [0, 4], [4, 6]]
+EARLY_EXPERTS = [[0, 1, 2, 4, 6], [0, 2, 4, 6], [0, 2, 4], [4, 6]]
 EARLY = [e * C for e in EARLY_EXPERTS[LAST]]
 HELD = C
 
 WHOLE = [(0, 112)]
 SHORT = [(0, 4), (32, 36), (36, 100)]
 MOVES = [[WHOLE, WHOLE, WHOLE], [SHORT, WHOLE, WHOLE], [WHOLE, SHORT, SHORT]]
+
+
+def pieces(a, m):
+    return [(0, LAST_CUT), (LAST_CUT, RANK_T)] if (a, m) == (LAST, R - 1) else [(0, RANK_T)]
 
 
 def tile_moe_eps_lin_silu_kernel(tc, xT, w_words, w_scales, b, offs, out):
@@ -53,10 +58,11 @@ def tile_moe_eps_lin_silu_kernel(tc, xT, w_words, w_scales, b, offs, out):
 
         offsets = keep.tile([P, S // LIST_GROUP], U16, name="offsets")
         bias = keep.tile([P, E], F32, name="bias")
-        raw = [
-            [keep.tile([P, PACK, RANK_T], F32, name="raw%d_%d" % (a, m), align_bytes=64) for m in range(R)]
-            for a in range(PASSES)
-        ]
+        raw = {}
+        for a in range(PASSES):
+            for m in range(R):
+                for lo, hi in pieces(a, m):
+                    raw[a, m, lo] = keep.tile([P, PACK, hi - lo], F32, name="raw%d_%d_%d" % (a, m, lo), align_bytes=64)
         grouped = [keep.tile([P, T, PACK], BF16, name="grouped%d" % a, align_bytes=64) for a in range(PASSES)]
         codes = [keep.tile([P, T], U32, name="codes%d" % a, align_bytes=64) for a in range(PASSES)]
         scales = keep.tile([P, T + U], U8, name="scales", align_bytes=64)
@@ -75,7 +81,8 @@ def tile_moe_eps_lin_silu_kernel(tc, xT, w_words, w_scales, b, offs, out):
         for a in range(PASSES):
             rows = xT[a * K_PASS:(a + 1) * K_PASS, :].rearrange("(p j) t -> p j t", j=PACK)
             for m in range(R):
-                nc.sync.dma_start(out=raw[a][m][:], in_=rows[:, :, m * RANK_T:(m + 1) * RANK_T])
+                for lo, hi in pieces(a, m):
+                    nc.sync.dma_start(out=raw[a, m, lo][:], in_=rows[:, :, m * RANK_T + lo:m * RANK_T + hi])
                 if a == 0 and m == 0:
                     nc.sync.dma_start(offsets[:], offs)
         nc.sync.dma_start(out=bias[:], in_=b)
@@ -94,9 +101,13 @@ def tile_moe_eps_lin_silu_kernel(tc, xT, w_words, w_scales, b, offs, out):
                 nc.sync.dma_start(out=matrix_words[:, matrices, :].bitcast(I32), in_=word_rows[:, matrices, :])
             return matrix_words
 
+        def loaded(a, m, lo, hi):
+            first = max(x for x, y in pieces(a, m) if x <= lo)
+            return raw[a, m, first][:, :, lo - first:hi - first]
+
         def cast(a, m, lo, hi, on_vector):
             dst = grouped[a][:, m * RANK_T + lo:m * RANK_T + hi, :].rearrange("p (c i) j -> p c j i", i=4)
-            src = raw[a][m][:, :, lo:hi].rearrange("p j (c i) -> p c j i", i=4)
+            src = loaded(a, m, lo, hi).rearrange("p j (c i) -> p c j i", i=4)
             if on_vector:
                 nc.vector.tensor_copy(out=dst, in_=src)
             else:
@@ -160,21 +171,21 @@ def tile_moe_eps_lin_silu_kernel(tc, xT, w_words, w_scales, b, offs, out):
         waiting = []
         for a in range(PASSES):
             for m in range(R):
-                on_scalar, on_vector, quantised = FIRST_PASS if a == 0 else LATER_PASSES
+                cuts = FIRST_PASS if a == 0 else LAST_LOAD if (a, m) == (LAST, R - 1) else LATER_PASSES
+                on_scalar, on_vector, on_gpsimd, quantised = cuts
                 for lo, hi in on_scalar:
                     cast(a, m, lo, hi, False)
                 for lo, hi in on_vector:
                     cast(a, m, lo, hi, True)
-                if a > 0:
-                    lo, hi = ON_GPSIMD
+                for lo, hi in on_gpsimd:
                     nc.gpsimd.tensor_copy(
                         out=grouped[a][:, m * RANK_T + lo:m * RANK_T + hi, :],
-                        in_=raw[a][m][:, :, lo:hi].rearrange("p j t -> p t j"),
+                        in_=loaded(a, m, lo, hi).rearrange("p j t -> p t j"),
                     )
                 for lo, hi in quantised:
                     quantize(a, m, lo, hi)
                 if waiting:
-                    gather_words(*waiting.pop(), tag="raw%d_%d" % (a, m))
+                    gather_words(*waiting.pop(), tag="raw%d_%d_%d" % (a, m, pieces(a, m)[-1][0]))
                 if a == LAST and m == 0:
                     for i, first in enumerate(EARLY):
                         gather(slot_scales[0][:, i * U:(i + 1) * U], scales[:, 0:RANK_T], first, first + U)

from contextlib import ExitStack

import concourse.mybir as mybir

K, T, E, C, N, R = 2048, 1280, 8, 256, 128, 2
S = E * C
FLOPS = 2 * K * N * S

F32 = mybir.dt.float32
BF16 = mybir.dt.bfloat16
I32 = mybir.dt.int32
U32 = mybir.dt.uint32
U16 = mybir.dt.uint16
U8 = mybir.dt.uint8
FP8X4 = mybir.dt.float8_e4m3fn_x4
FP4X4 = mybir.dt.float4_e2m1fn_x4
ACT = mybir.ActivationFunctionType

P = 128
PACK = 4
K_PASS = P * PACK
PASSES = K // K_PASS
LAST = PASSES - 1
RANK_T = T // R
U = C // R
PAIR = 2 * C
PAIRS = E // 2
LATE = PAIR - U
HALF = S // 2
LIST_GROUP = 16
QUADRANT = 32
SCALE_ROWS = 4
LAST_GATHER = T // 8

FIRST_PASS = ([(0, 256)], [(256, 512), (512, 640)], [], [(256, 512), (0, 256), (512, 640)])
LATER_PASSES = ([(0, 352), (512, 640)], [], [(352, 512)], [(0, 512), (512, 640)])
LAST_CUT = 384
LAST_LOAD = ([(0, 256), (256, 384), (384, 512), (512, 640)], [], [], [(0, 256), (256, 512), (512, 640)])

EARLY_EXPERTS = [[0, 1, 2, 4, 6], [0, 2, 4, 6], [0, 2, 4], [4, 6]]
EARLY = [e * C for e in EARLY_EXPERTS[LAST]]
HELD = C

WHOLE = [(0, 112)]
SHORT = [(0, 4), (32, 36), (36, 100)]
MOVES = [[WHOLE, WHOLE, WHOLE], [SHORT, WHOLE, WHOLE], [WHOLE, SHORT, SHORT]]


def pieces(a, m):
    return [(0, LAST_CUT), (LAST_CUT, RANK_T)] if (a, m) == (LAST, R - 1) else [(0, RANK_T)]


def tile_moe_eps_lin_silu_kernel(tc, xT, w_words, w_scales, b, offs, out):
    nc = tc.nc
    with ExitStack() as ctx:
        keep = ctx.enter_context(tc.tile_pool(name="keep", bufs=1))
        psum = ctx.enter_context(tc.psum_pool(name="psum", bufs=1))

        offsets = keep.tile([P, S // LIST_GROUP], U16, name="offsets")
        bias = keep.tile([P, E], F32, name="bias")
        raw = {}
        for a in range(PASSES):
            for m in range(R):
                for lo, hi in pieces(a, m):
                    raw[a, m, lo] = keep.tile([P, PACK, hi - lo], F32, name="raw%d_%d_%d" % (a, m, lo), align_bytes=64)
        grouped = [keep.tile([P, T, PACK], BF16, name="grouped%d" % a, align_bytes=64) for a in range(PASSES)]
        codes = [keep.tile([P, T], U32, name="codes%d" % a, align_bytes=64) for a in range(PASSES)]
        scales = keep.tile([P, T + U], U8, name="scales", align_bytes=64)
        widths = [len(EARLY) * U, HALF, 2 * LATE]
        slot_scales = [keep.tile([P, w], U8, name="slot_scales%d" % i, align_bytes=64) for i, w in enumerate(widths)]
        moved = [keep.tile([P, LAST, w], U8, name="moved%d" % i, align_bytes=64) for i, w in enumerate(widths)]
        w_planes = keep.tile([P, E * PASSES, N], U8, name="w_planes", align_bytes=64)
        result = keep.tile([P, R, E * U], F32, name="result")
        banks = [psum.tile([P, C], F32, name="bank%d" % e) for e in range(E)]

        nc.vector.memset(scales[:].bitcast(I32), 0)
        nc.vector.memset(w_planes[:].bitcast(I32), 0)
        for planes in moved:
            nc.vector.memset(planes[:].bitcast(I32), 0)

        for a in range(PASSES):
            rows = xT[a * K_PASS:(a + 1) * K_PASS, :].rearrange("(p j) t -> p j t", j=PACK)
            for m in range(R):
                for lo, hi in pieces(a, m):
                    nc.sync.dma_start(out=raw[a, m, lo][:], in_=rows[:, :, m * RANK_T + lo:m * RANK_T + hi])
                if a == 0 and m == 0:
                    nc.sync.dma_start(offsets[:], offs)
        nc.sync.dma_start(out=bias[:], in_=b)
        scale_rows = w_scales.rearrange("e a q n -> q (e a) n").bitcast(I32)
        for quad in range(P // QUADRANT):
            nc.sync.dma_start(
                out=w_planes[QUADRANT * quad:QUADRANT * quad + SCALE_ROWS].bitcast(I32),
                in_=scale_rows[SCALE_ROWS * quad:SCALE_ROWS * (quad + 1)],
            )

        def load_words():
            matrix_words = keep.tile([P, E * PASSES, 2 * N], U8, name="w_codes", tag="grouped1", align_bytes=64)
            word_rows = w_words.rearrange("e a p c -> p (e a) c").bitcast(I32)
            for pair in range(PAIRS):
                matrices = slice(2 * pair * PASSES, 2 * (pair + 1) * PASSES)
                nc.sync.dma_start(out=matrix_words[:, matrices, :].bitcast(I32), in_=word_rows[:, matrices, :])
            return matrix_words

        def loaded(a, m, lo, hi):
            first = max(x for x, y in pieces(a, m) if x <= lo)
            return raw[a, m, first][:, :, lo - first:hi - first]

        def cast(a, m, lo, hi, on_vector):
            dst = grouped[a][:, m * RANK_T + lo:m * RANK_T + hi, :].rearrange("p (c i) j -> p c j i", i=4)
            src = loaded(a, m, lo, hi).rearrange("p j (c i) -> p c j i", i=4)
            if on_vector:
                nc.vector.tensor_copy(out=dst, in_=src)
            else:
                nc.scalar.activation(out=dst, in_=src, func=ACT.Copy)

        def quantize(a, m, lo, hi):
            cols = slice(m * RANK_T + lo, m * RANK_T + hi)
            nc.vector.quantize_mx(
                out=codes[a][:, cols].bitcast(FP8X4),
                scales=scales[SCALE_ROWS * a:P, cols],
                in_=grouped[a][:, cols, :].rearrange("p t j -> p (t j)"),
            )

        def gather(dst, window, lo, hi):
            nc.vector.tensor_copy(dst, window.indirect(offsets[:, lo // LIST_GROUP:hi // LIST_GROUP]))

        slot_words = {}

        def words_tile(a, lo, hi, tag=""):
            piece = keep.tile([P, hi - lo], U32, name="words%d_%d" % (a, lo), tag=tag, align_bytes=64)
            for first in range(lo, hi, U):
                slot_words[a, first] = piece[:, first - lo:first - lo + U]
            return piece

        def gather_words(a, lo, hi, tag=""):
            rank0_alone = hi - lo == U and lo % C == 0
            gather(words_tile(a, lo, hi, tag)[:], codes[a][:, 0:RANK_T] if rank0_alone else codes[a][:], lo, hi)

        def late_runs(a, lo, hi):
            edges = [lo] + [x for e in EARLY_EXPERTS[a] if lo <= e * C < hi for x in (e * C, e * C + U)] + [hi]
            return [(x, y) for x, y in zip(edges[0::2], edges[1::2]) if x < y]

        def move_planes(i):
            for a in range(1, PASSES):
                for lo, hi in MOVES[i][a - 1]:
                    nc.sync.dma_start(
                        out=moved[i][lo:hi, a - 1, :].bitcast(I32),
                        in_=slot_scales[i][SCALE_ROWS * a + lo:SCALE_ROWS * a + hi, :].bitcast(I32),
                    )

        def plane(e, m, a):
            first = e * C + m * U
            if first in EARLY:
                i, col = 0, EARLY.index(first) * U
            else:
                i = 1 + first // HALF
                col = first % HALF - U * len([x for x in EARLY if first // HALF * HALF <= x < first])
            return slot_scales[i][:, col:col + U] if a == 0 else moved[i][:, a - 1, col:col + U]

        def multiply(e, m, a):
            nc.tensor.matmul_mx(
                out=banks[e][:, m * U:(m + 1) * U],
                lhsT=w_codes[:, e * PASSES + a, :].bitcast(FP4X4),
                lhsT_scale=w_planes[:, e * PASSES + a, :],
                rhs=slot_words[a, e * C + m * U].bitcast(FP8X4),
                rhs_scale=plane(e, m, a),
                start=(a == 0 and m == (1 if e * C in EARLY else 0)),
                stop=(a == LAST and m == R - 1),
            )

        waiting = []
        for a in range(PASSES):
            for m in range(R):
                cuts = FIRST_PASS if a == 0 else LAST_LOAD if (a, m) == (LAST, R - 1) else LATER_PASSES
                on_scalar, on_vector, on_gpsimd, quantised = cuts
                for lo, hi in on_scalar:
                    cast(a, m, lo, hi, False)
                for lo, hi in on_vector:
                    cast(a, m, lo, hi, True)
                for lo, hi in on_gpsimd:
                    nc.gpsimd.tensor_copy(
                        out=grouped[a][:, m * RANK_T + lo:m * RANK_T + hi, :],
                        in_=loaded(a, m, lo, hi).rearrange("p j t -> p t j"),
                    )
                for lo, hi in quantised:
                    quantize(a, m, lo, hi)
                if waiting:
                    gather_words(*waiting.pop(), tag="raw%d_%d_%d" % (a, m, pieces(a, m)[-1][0]))
                if a == LAST and m == 0:
                    for i, first in enumerate(EARLY):
                        gather(slot_scales[0][:, i * U:(i + 1) * U], scales[:, 0:RANK_T], first, first + U)
                    move_planes(0)
                if a == 1 and m == R - 1:
                    w_codes = load_words()
                runs = []
                if m == 0:
                    runs = [(e * C, e * C + U) for e in EARLY_EXPERTS[a]]
                elif a < LAST:
                    runs = late_runs(a, 0, S - HELD if a == LAST - 1 else S)
                if m == 0 or a < LAST - 1:
                    waiting.append((a, *runs.pop()))
                for lo, hi in runs:
                    gather_words(a, lo, hi)

        out_by_rank = out.rearrange("n (m x) -> n m x", m=R)

        def gather_late_scales(half):
            at = 0
            for lo, hi in late_runs(LAST, half * HALF, (half + 1) * HALF):
                gather(slot_scales[1 + half][:, at:at + hi - lo], scales[:], lo, hi)
                at = at + hi - lo
            move_planes(1 + half)

        def multiply_late(pairs, passes):
            for a in passes:
                for pair in pairs:
                    for first in range(pair * PAIR + (U if pair * PAIR in EARLY else 0), (pair + 1) * PAIR, U):
                        multiply(first // C, (first // U) % R, a)

        def open_half(half):
            multiply_late([2 * half, 2 * half + 1], [0])
            for a in range(PASSES):
                for first in EARLY:
                    if first // HALF == half:
                        multiply(first // C, 0, a)

        def activate(e):
            nc.scalar.activation(
                out=result[:, :, e * U:(e + 1) * U],
                in_=banks[e][:].rearrange("p (m u) -> p m u", m=R),
                func=ACT.Silu,
                bias=bias[:, e:e + 1],
            )

        def store(e_lo, e_hi):
            cols = slice(e_lo * U, e_hi * U)
            nc.sync.dma_start(out=out_by_rank[:, :, cols], in_=result[:, :, cols])

        def close_pair(pair):
            gather_words(LAST, pair * PAIR + (U if pair * PAIR in EARLY else 0), (pair + 1) * PAIR)
            if pair * PAIR not in EARLY:
                multiply(2 * pair, 0, LAST)
            multiply(2 * pair, 1, LAST)
            activate(2 * pair)
            multiply(2 * pair + 1, 0, LAST)
            multiply(2 * pair + 1, 1, LAST)
            activate(2 * pair + 1)
            store(2 * pair, 2 * pair + 2)

        gather_late_scales(0)
        open_half(0)
        gather_late_scales(1)
        open_half(1)
        multiply_late([0, 1], [1, 2])
        close_pair(0)
        close_pair(1)
        multiply_late([2, 3], [1])
        gather_words(LAST - 1, S - HELD, S, tag="grouped%d" % LAST)
        multiply_late([2, 3], [2])
        close_pair(2)

        cut = S - LAST_GATHER
        words = words_tile(LAST, S - LATE, S)
        gather(words[:, 0:LATE - LAST_GATHER], codes[LAST][:], S - LATE, cut)
        multiply(E - 2, 1, LAST)
        activate(E - 2)
        store(E - 2, E - 1)
        gather(words[:, LATE - LAST_GATHER:], codes[LAST][:], cut, S)
        e = E - 1
        for m in range(R):
            multiply(e, m, LAST)
        for m in range(R):
            nc.scalar.activation(
                out=result[:, m, e * U:], in_=banks[e][:, m * U:(m + 1) * U], func=ACT.Silu, bias=bias[:, e:e + 1]
            )
            nc.sync.dma_start(out=out_by_rank[:, m, e * U:], in_=result[:, m, e * U:])
